import numpy as np, ml_dtypes
CORES = [23,119,17,113]
N = 4
BF = ml_dtypes.bfloat16
def f(rng, *shape):
    return (rng.standard_normal(shape, dtype=np.float32) * np.exp2(rng.integers(-2, 3, shape[:-1] + (1,)))).astype(BF)
def wide(rng, *shape):
    v = f(rng, *shape).astype(np.float32); k = shape[:-2] + (1, shape[-1])
    return (v * np.exp2(rng.integers(-6, 7, k)) * (rng.random(k) > 0.0625)).astype(BF)
def gentries(a):
    return np.ascontiguousarray(a.reshape(8, 16, -1).transpose(0, 2, 1)).reshape(8, -1)
def gtable(e):
    e = np.asarray(e); return np.ascontiguousarray(e.reshape(8, -1, 16).transpose(0, 2, 1)).reshape(128, -1).astype(np.int32)
E, M, CAPP, R = 4096, 4928, 128, 2
GX, GY, GZ = 16, 16, 16
def mesh(rng):
    return np.stack([np.stack([rng.permutation(M)[:E] for c in range(8)]) for r in range(N)])
def counts(rng, lo):
    n = np.triu(rng.integers(lo, CAPP + 1, (N, N)), 1); r = int(rng.integers(0, N - 1)); n[r, int(rng.integers(r + 1, N))] = CAPP; return n
def several(rng, k):
    return [sorted(rng.choice(N, int(j), replace=False).tolist()) for j in rng.integers(3, N + 1, k)]
def shares(rng, num, sets, pool):
    h = np.tile(M + np.arange(CAPP), (N, 8, 1)); left = np.array(num); at = [0] * N; same = []
    free = {(r, q): rng.permutation(CAPP).tolist() for r in range(N) for q in range(r + 1, N)}
    def join(S):
        n = [int(pool[r][at[r]]) for r in S]
        for i, r in enumerate(S):
            at[r] += 1
            for j in range(i + 1, len(S)):
                q = S[j]; k = free[r, q].pop(); h[r, q, k] = n[i]; h[q, r, k] = n[j]; left[r, q] -= 1
            if i: same.append((S[0], n[0], r, n[i]))
    for S in sets:
        if all(left[S[i], S[j]] > 0 for i in range(len(S)) for j in range(i + 1, len(S))): join(S)
    for r in range(N):
        for q in range(r + 1, N):
            for i in range(int(left[r, q])): join([r, q])
    return h, same
def make(rng, c, hs, u, st):
    h, same = hs; w = ((0.5 + rng.random((N, 1, M))) * 0.125).astype(BF); u = np.array(u)
    for r, n, q, m in same:
        u[q, :, m] = u[r, :, n]; w[q, 0, m] = w[r, 0, n]
    return {"u": u, "w": w, "ke": rng.standard_normal((N, 8, 8)).astype(BF), "st": st.astype(BF), "conn": np.stack([gtable(a) for a in c]), "share": np.stack([gtable(a) for a in h])}
def setup_inputs(rng):
    c = mesh(rng); hs = shares(rng, counts(rng, CAPP // 2), several(rng, CAPP // 2), [rng.permutation(M) for r in range(N)])
    return make(rng, c, hs, f(rng, N, 16, M), 0.5 + rng.random((N, 1, E)))
def setup_inputs_grid(rng):
    e = np.arange(E); x, y, z = e % GX, e // GX % GY, e // (GX * GY)
    c = np.stack([((z + (k >> 2)) * (GY + 1) + y + (k >> 1 & 1)) * (GX + 1) + x + (k & 1) for k in range(8)])
    n = np.arange((GX + 1) * (GY + 1) * (GZ + 1)); x, y, z = n % (GX + 1), n // (GX + 1) % (GY + 1), n // ((GX + 1) * (GY + 1))
    n = n[(x == 0) | (x == GX) | (y == 0) | (y == GY) | (z == 0) | (z == GZ)]
    b = rng.integers(0, M - (GX + 1) * (GY + 1) * (GZ + 1) + 1, N)
    hs = shares(rng, counts(rng, 1), several(rng, CAPP // 4), [b[r] + rng.permutation(n) for r in range(N)])
    return make(rng, np.stack([c + b[r] for r in range(N)]), hs, f(rng, N, 16, M), 0.5 + rng.random((N, 1, E)))
def setup_inputs_all(rng):
    hs = shares(rng, np.triu(np.full((N, N), CAPP), 1), [list(range(N))] * CAPP, [rng.permutation(M) for r in range(N)])
    return make(rng, mesh(rng), hs, f(rng, N, 16, M), 0.5 + rng.random((N, 1, E)))
def setup_inputs_few(rng):
    n = np.zeros((N, N), np.int64)
    for q in range(1, N): n[q - 1, q] = rng.integers(0, 4)
    r = int(rng.integers(0, N - 1)); q = int(rng.integers(r + 1, N)); n[r, q] = CAPP
    inner = np.arange(1, M - 1); pool = [np.concatenate([[0, M - 1], rng.permutation(inner)]) for k in range(N)]
    c = np.zeros((N, 8, E), np.int64)
    for k in range(N):
        for a in range(8): c[k, a] = np.concatenate([[M - 1 if a % 2 else 0], rng.permutation(inner)[:E - 2], [0 if a % 2 else M - 1]])
    k = (r, q)[int(rng.integers(0, 2))]; c[k] = c[k, :1]
    return make(rng, c, shares(rng, n, [], pool), f(rng, N, 16, M), 0.5 + rng.random((N, 1, E)))
def setup_inputs_spread(rng):
    c = mesh(rng); hs = shares(rng, counts(rng, CAPP // 4), several(rng, CAPP), [rng.permutation(M) for r in range(N)])
    return make(rng, c, hs, wide(rng, N, 16, M), np.exp2(rng.integers(-2, 3, (N, 1, E))) * (rng.random((N, 1, E)) > 0.0625))
def check_inputs(d):
    bad = []; c = np.stack([gentries(a) for a in d["conn"]]).astype(np.int64); h = np.stack([gentries(a) for a in d["share"]]).astype(np.int64)
    if not all(np.isfinite(d[k].astype(np.float32)).all() for k in ("u", "w", "ke", "st")): bad.append("finite")
    if c.min() < 0 or c.max() >= M: bad.append("conn_in_range")
    t = np.sort(c, -1)
    if (t[..., 1:] == t[..., :-1]).any(): bad.append("a_node_is_corner_c_of_one_element_at_most")
    used = (h >= 0) & (h < M)
    if not (used | (h == M + np.arange(CAPP))).all(): return bad + ["share_in_range"]
    t = np.sort(h, -1)
    if (t[..., 1:] == t[..., :-1]).any(): return bad + ["a_node_stands_once_in_a_pairs_slots"]
    if used[:, N:].any() or any(used[r, r].any() for r in range(N)): return bad + ["own_and_unused_groups_empty"]
    if not (used[:, :N] == used[:, :N].transpose(1, 0, 2)).all(): return bad + ["slots_in_use_on_both_sides"]
    cp = np.full((N, M, N), -1, np.int64); alike = True
    for r in range(N):
        cp[r, :, r] = np.arange(M)
        for q in range(N):
            if q != r:
                k = used[r, q]; a, b = h[r, q][k], h[q, r][k]; cp[r, a, q] = b
                alike = alike and bool((d["u"][r][:, a] == d["u"][q][:, b]).all() and (d["w"][r][:, a] == d["w"][q][:, b]).all())
    if not alike: bad.append("copies_alike")
    if not all((cp[r, h[r, q][used[r, q]]] == cp[q, h[q, r][used[q, r]]]).all() for r in range(N) for q in range(N) if q != r): bad.append("all_copies_listed")
    return bad
def reference(u, w, ke, st, conn, share):
    c = [gentries(a) for a in conn]; h = [gentries(a) for a in share]
    x = u.astype(np.float64); wt = w.astype(np.float64); km = ke.astype(np.float64); sf = st.astype(np.float64)
    for t in range(R):
        p = np.zeros((N, 16, M + CAPP), np.float64)
        for r in range(N):
            v = np.einsum('ab,lbe->lae', km[r], x[r][:, c[r]]) * sf[r]
            for a in range(8): p[r][:, c[r][a]] += v[:, a]
        z = np.array(p)
        for r in range(N):
            for q in range(N):
                if q != r: z[r][:, h[r][q]] += p[q][:, h[q][r]]
        x = x - wt * z[:, :, :M]
    return {"y": x.astype(np.float32)}

@@ -1,0 +1,441 @@
+import numpy as np
+from concourse.bass import DstId, RemoteDMATransfer, IndirectOffsetOnAxis
+from concourse.mybir import dt, AluOpType, AxisListType, ActivationFunctionType
+
+A = AluOpType
+F = ActivationFunctionType
+E, M, CAPP = 4096, 4928, 128
+MW = M + CAPP
+RUN = MW // 16
+NK = M // 16
+ES = 2304
+CB = 640
+YW = CB + CAPP
+PER = 4
+
+_F = "float32 "
+_B = "bfloat16 "
+_I = "int32 "
+_U = "uint16 "
+_SB = {
+    256: _I + "connI piI " + _U + "connU piU " + _F + "piN piT",
+    MW: _B + "uwin wrep " + _F + "Wv Ws win ADD",
+    E: _B + "strep X1 " + _F + "X2", ES: _F + "dat", E + 8: _F + "V", 8 * CB: _F + "G",
+    NK: _F + "invV invS invT", 320: _U + "invU invP",
+    128: _I + "idm idt asI asJ " + _F + "PosR NegR IdF KlF Rw " + _B + "IdB asB Yb KlB",
+    2: _I + "pI g16 zI", 8: _F + "mk " + _B + "keB " + _I + "shI " + _U + "shU",
+    24: _F + "shM SRf sqN sqT dmp0 dmp c1 c2 c3 c4 " + _I + "SRi sqI " + _U + "SRu piS clU cpU",
+    384: _F + "O1 O2 Om uslot wslot S1 D1 x2s x3s", 48: _F + "send1 send2", 64: _F + "recv1 recv2",
+    CB: _B + "wc wT " + _F + "x2c xT yt yu", YW: _F + "Y",
+}
+SCRATCH = {}
+for _n in _SB:
+    _t = ""
+    for _w in _SB[_n].split():
+        if _w + " " in (_F, _B, _I, _U):
+            _t = _w
+        else:
+            SCRATCH[_w] = ("sbuf", [128, _n], _t)
+for _k in range(8):
+    SCRATCH["pb%d" % _k] = ("psum", [128, 512], "float32")
+
+SEMAPHORES = ["cv", "cs", "ct", "cg", "dconn", "dshare", "dke", "du", "dstr", "dwr", "dxv", "dxs", "dwc", "dx2", "dy",
+              "arr1", "arr2", "loc1", "loc2"]
+
+
+def rank_program(g, core, T, topo):
+    r = T.rank_of(core)
+    if r is None:
+        return
+    partners = [q for q in range(len(T.cores)) if q != r]
+    queue = {"v": g.vector, "s": g.scalar, "t": g.tensor, "g": g, "y": g.sync}
+    count = {}
+    seen = {}
+    past = {}
+
+    def wait(q, toks):
+        best = {}
+        for name, val in toks:
+            best[name] = max(best.get(name, 0), val)
+        for name in sorted(best):
+            if seen.get((q, name), 0) < best[name]:
+                queue[q].wait_ge(T.sem[name], int(best[name]))
+                seen[(q, name)] = best[name]
+
+    def needs(q, R, W, own, acc):
+        toks = []
+        for lst, wr in ((R, False), (W, True)):
+            for name, lo, hi in lst:
+                psum = name[:2] == "pb"
+                for (l2, h2, w2, sem, val, q2) in past.get(name, []):
+                    if sem == own and own[:1] == "d":
+                        continue
+                    same = q2 == q and sem[:1] == "c"
+                    if psum and not same:
+                        hit = True
+                    else:
+                        hit = l2 < hi and lo < h2 and (w2 or wr)
+                        if same and (not w2 or (wr and acc)):
+                            hit = False
+                    if hit:
+                        toks.append((sem, count[sem] if sem[:1] == "d" else val))
+        return toks
+
+    def record(q, R, W, sem, val):
+        for lst, wr in ((R, False), (W, True)):
+            for name, lo, hi in lst:
+                old = past.get(name, [])
+                if name[:2] == "pb":
+                    old = [a for a in old if a[5] == q]
+                elif wr:
+                    old = [a for a in old if not (lo <= a[0] and a[1] <= hi and not (a[3] == sem and sem[:1] == "d"))]
+                past[name] = old + [(lo, hi, wr, sem, val, q)]
+
+    def op(q, fn, R=(), W=(), acc=False, extra=()):
+        sem = "c" + q
+        wait(q, needs(q, R, W, sem, acc) + list(extra))
+        fn(queue[q]).then_inc(T.sem[sem], 1)
+        count[sem] = count.get(sem, 0) + 1
+        record(q, R, W, sem, count[sem])
+
+    def dma(q, sem, fn, R=(), W=()):
+        wait(q, needs(q, R, W, sem, False))
+        fn(queue[q]).then_inc(T.sem[sem], 16)
+        count[sem] = count.get(sem, 0) + 16
+        record(q, R, W, sem, count[sem])
+
+    def a(name, lo=0, hi=None):
+        return (name, lo, SCRATCH[name][1][1] if hi is None else hi)
+
+    def ap(x):
+        return T[x[0]][:, x[1]:x[2]]
+
+    def fill(x, val):
+        op("v", lambda e: e.memset(ap(x), val), W=[x])
+
+    def ts(out, in0, s1, op0, s2=None, op1=None, R=()):
+        if op1 is None:
+            op("v", lambda e: e.tensor_scalar(ap(out), ap(in0), s1, None, op0), R=[in0] + list(R), W=[out])
+        else:
+            op("v", lambda e: e.tensor_scalar(ap(out), ap(in0), s1, s2, op0, op1), R=[in0] + list(R), W=[out])
+
+    def tt(out, in0, in1, o):
+        op("v", lambda e: e.tensor_tensor(ap(out), ap(in0), ap(in1), o), R=[in0, in1], W=[out])
+
+    def cp(out, in_):
+        op("v", lambda e: e.tensor_copy(ap(out), ap(in_)), R=[in_], W=[out])
+
+    def scp(out, in_, func=F.Copy, scale=1.0):
+        op("s", lambda e: e.activation(ap(out), ap(in_), func, scale=scale), R=[in_], W=[out])
+
+    def gat(q, out, win, off):
+        if q == "v":
+            op("v", lambda e: e.tensor_copy(ap(out), ap(win).indirect(ap(off))), R=[win, off], W=[out])
+        else:
+            op("s", lambda e: e.activation(ap(out), ap(win).indirect(ap(off)), F.Copy), R=[win, off], W=[out])
+
+    def gtt(out, win, off, in1, o):
+        op("v", lambda e: e.tensor_tensor(ap(out), ap(win).indirect(ap(off)), ap(in1), o), R=[win, off, in1], W=[out])
+
+    def sca(win, off, in_):
+        op("v", lambda e: e.tensor_copy(ap(win).indirect(ap(off)), ap(in_)), R=[off, in_], W=[win])
+
+    def mm(out, lhsT, rhs, start, stop):
+        op("t", lambda e: e.matmul(ap(out), ap(lhsT), ap(rhs), start, stop), R=[lhsT, rhs], W=[out], acc=not start)
+
+    def iota(out, pattern, base, cm, imprecise=False):
+        if imprecise:
+            op("g", lambda e: e.iota(ap(out), pattern, base, cm, allow_small_or_imprecise_dtypes=True), W=[out])
+        else:
+            op("g", lambda e: e.iota(ap(out), pattern, base, cm), W=[out])
+
+    def broadcast(sem, out, row):
+        dma("g", sem, lambda e: e.indirect_dma_start(ap(out), None, T[row][:], IndirectOffsetOnAxis(ap=T.zI[:, 0:1], axis=0),
+                                                     bounds_check=0), R=[a("zI")], W=[out])
+
+    dma("y", "dconn", lambda e: e.dma_start(T.connI[:], T.conn[:]), W=[a("connI")])
+    dma("y", "dshare", lambda e: e.dma_start(T.shI[:], T.share[:]), W=[a("shI")])
+    dma("y", "dke", lambda e: e.dma_start(T.keB[0:8, :], T.ke[:]), W=[a("keB")])
+    for c in range(8):
+        dma("y", "du", lambda e, c=c: e.dma_start(T.uwin[16 * c:16 * c + 16, 0:M], T.u[:]), W=[a("uwin", 0, M)])
+
+    H, W3, S3 = 632, 3 * (MW // 4), MW - 632
+    fill(a("Wv", 0, H), 0.0)
+    fill(a("zI"), 0)
+    iota(a("dat", 0, 1024), [[-1, 1024]], E, 0, True)
+    iota(a("Wv", W3, MW), [[0, MW - W3]], 0, 0, True)
+    iota(a("Ws", S3, MW), [[0, MW - S3]], 0, 0, True)
+    iota(a("dat", 1024, 2048), [[-1, 1024]], E - 1024, 0, True)
+    broadcast("dstr", a("strep"), "st")
+    iota(a("idm"), [[-1, 128]], 128, 1)
+    iota(a("pI"), [[0, 2]], 0, 1)
+    op("g", lambda e: e.iota(T.asI[0:8, :], [[1, 128]], 128, -16), W=[a("asI")])
+    iota(a("dmp0"), [[0, 3], [16, 8]], CB, 1, True)
+    iota(a("dat", 2048, ES), [[-1, ES - 2048]], E - 2048, 0, True)
+    broadcast("dwr", a("wrep", 0, M), "w")
+    iota(a("ADD", 0, MW // 2), [[0, MW // 2]], 0, 0, True)
+
+    scp(a("Ws", 0, H), a("Wv", 0, H), F.Silu)
+    for lo, hi in ((H, 2 * H), (2 * H, 4 * H), (4 * H, S3)):
+        scp(a("Ws", lo, hi), a("Ws", 0, hi - lo), F.Silu)
+    fill(a("Wv", H, 4 * H), 0.0)
+
+    def runs(out, src, i_, n_, t_):
+        ts(i_, src, 15, A.bitwise_and)
+        ts(n_, src, 1.0 / (16 * RUN - 1), A.mult)
+        tt(t_, n_, i_, A.add)
+        ts(out, t_, (16 * RUN - 1) / 16.0, A.mult, 0.25, A.add)
+
+    runs(a("piU"), a("connI"), a("piI"), a("piN"), a("piT"))
+    fill(a("Wv", 4 * H, W3), 0.0)
+
+    def scat_s(e0, e1):
+        off, x = a("piU", e0 // 16, e1 // 16), a("dat", e0, e1)
+        op("s", lambda e: e.activation(ap(a("Ws")).indirect(ap(off)), ap(x), F.Silu), R=[off, x], W=[a("Ws")])
+
+    def scat_v(e0, e1):
+        off, x = a("piU", e0 // 16, e1 // 16), a("dat", e0 - ES, e1 - ES)
+        op("v", lambda e: e.tensor_scalar(ap(a("Wv")).indirect(ap(off)), ap(x), 1.0, float(-ES), A.mult, A.add),
+           R=[off, x], W=[a("Wv")])
+
+    scat_s(0, 1024)
+    scat_v(ES, ES + 1024)
+    scat_s(1024, 2048)
+    scat_v(ES + 1024, E)
+    scat_s(2048, ES)
+    for nm, wn, sem in (("invV", "Wv", "dxv"), ("invS", "Ws", "dxs")):
+        for i in range(16):
+            dma("y", sem, lambda e, i=i, nm=nm, wn=wn: e.dma_start(T[nm][i:128:16, :], T[wn][i:128:16, RUN * i:RUN * i + NK]),
+                R=[a(wn)], W=[a(nm)])
+
+    cp(a("connU"), a("connI"))
+    op("v", lambda e: e.tensor_scalar(T.asJ[0:8, :], T.asI[0:8, :], 4, None, A.arith_shift_right), R=[a("asI")], W=[a("asJ")])
+    ts(a("idt"), a("idm"), 15, A.bitwise_and)
+    op("v", lambda e: e.tensor_scalar(T.asB[0:8, :], T.asJ[0:8, :], 8, None, A.is_equal), R=[a("asJ")], W=[a("asB")])
+    op("t", lambda e: e.matmul(T.pb1[0:8, 0:128], T.keB[0:8, 0:8], T.asB[0:8, :], True, True),
+       R=[a("keB"), a("asB")], W=[a("pb1", 0, 128)])
+    ts(a("PosR"), a("idt"), 0, A.is_equal)
+    ts(a("g16"), a("pI"), 4, A.arith_shift_right)
+    op("v", lambda e: e.tensor_copy(T.Yb[0:8, :], T.pb1[0:8, 0:128]), R=[a("pb1", 0, 128)], W=[a("Yb")])
+    op("t", lambda e: e.matmul(T.pb2[:, 0:128], T.asB[0:8, :], T.Yb[0:8, :], True, True),
+       R=[a("asB"), a("Yb")], W=[a("pb2", 0, 128)])
+    for k, q in enumerate(partners):
+        ts(a("mk", k, k + 1), a("g16", 0, 1), q, A.is_equal)
+    tt(a("KlB"), a("pb2", 0, 128), a("PosR"), A.mult)
+    for k in range(3):
+        ts(a("shM", 8 * k, 8 * k + 8), a("shI"), T.mk[:, k:k + 1], A.mult, R=[a("mk", k, k + 1)])
+    mm(a("pb0", 0, 24), a("PosR"), a("shM"), True, True)
+    fill(a("uwin", M, MW), 0.0)
+    fill(a("wrep", M, MW), 0.0)
+    ts(a("IdF"), a("idm"), 128, A.is_equal)
+    cp(a("SRi"), a("pb0", 0, 24))
+    cp(a("SRu"), a("pb0", 0, 24))
+    runs(a("piS"), a("SRi"), a("sqI"), a("sqN"), a("sqT"))
+
+    gat("v", a("O1"), a("Wv"), a("piS"))
+    gtt(a("O2"), a("Ws"), a("piS"), a("O1"), A.add)
+    for k in range(3):
+        tt(a("Om", 128 * k, 128 * k + 128), a("O2", 128 * k, 128 * k + 128), a("PosR"), A.mult)
+
+    def comp_lists(i0, i1):
+        for i in range(i0, i1):
+            op("t", lambda e, i=i: e.matmul(T.pb3[:, 0:24], T.IdF[:], T.Om[:, i:384:16], i == 0, i == 15),
+               R=[a("IdF"), a("Om")], W=[a("pb3", 0, 24)], acc=i > 0)
+
+    def kmul(bank, K, X, x0, x1):
+        mm(a(bank, 0, x1 - x0), a(K), a(X, x0, x1), True, True)
+
+    def stmul(bank, x0, x1):
+        tt(a("V", x0, x1), a(bank, 0, x1 - x0), a("strep", x0, x1), A.mult)
+
+    for j in range(8):
+        x0, x1 = 512 * j, 512 * j + 512
+        bank = "pb%d" % (4 + j % 4)
+        gat("s", a("X1", x0, x1), a("uwin"), a("connU", 32 * j, 32 * j + 32))
+        kmul(bank, "KlB", "X1", x0, x1)
+        stmul(bank, x0, x1)
+        if j == 0:
+            tt(a("KlF"), a("pb2", 0, 128), a("PosR"), A.mult)
+            ts(a("IdB"), a("idm"), 128, A.is_equal)
+        if 1 <= j <= 4:
+            comp_lists(4 * j - 4, 4 * j)
+        if j == 1:
+            ts(a("NegR"), a("idt"), 0, A.is_equal, -1.0, A.mult)
+            fill(a("V", E, E + 8), 0.0)
+        if j == 2:
+            cp(a("shU"), a("shI"))
+            for k in (1, 2):
+                fill(a("recv%d" % k, 16 * r, 16 * r + 16), 0.0)
+        if j == 4:
+            tt(a("invT"), a("invV"), a("invS"), A.add)
+        if j == 5:
+            ts(a("invU", 0, NK), a("invT"), -1.0, A.mult, E + 0.25, A.add)
+            fill(a("invU", NK, 320), E)
+        if j == 6:
+            ts(a("clU"), a("pb3", 0, 24), -1.0, A.mult, E + 0.25, A.add)
+            for c in range(4):
+                mm(a("pb%d" % c), a("IdB"), a("uwin", 512 * c, 512 * c + 512), True, False)
+    gat("s", a("wslot"), a("wrep"), a("SRu"))
+    gat("s", a("uslot"), a("uwin"), a("SRu"))
+
+    VW = a("V")
+    FX = a("pb3", 0, 384)
+    used, masks = [], {}
+    for q in sorted(partners, key=lambda q: len(topo.engines(core, T.cores[q]))):
+        ok = [e for e in topo.engines(core, T.cores[q]) if e not in used][:PER]
+        used += ok
+        masks[q] = sum(1 << e for e in ok)
+
+    def slots():
+        gtt(a("S1"), VW, a("clU"), a("wslot"), A.mult)
+
+    def message():
+        for k in range(3):
+            mm(a("pb7", 16 * k, 16 * k + 16), a("S1", 128 * k, 128 * k + 128), a("PosR", 0, 16), True, True)
+
+    def send(rnd):
+        nm = "send%d" % rnd
+        wait("g", needs("g", [a(nm)], [], "loc%d" % rnd, False))
+        tr = []
+        for k, q in enumerate(partners):
+            rid, pid, _se = topo.addr(T.cores[q])
+            tr.append(RemoteDMATransfer(dst_ids=[DstId(rid=rid, pnc=pid)], dma_engine_mask=masks[q],
+                                        remote_sem=T.sem["arr%d" % rnd], src=T[nm][:, 16 * k:16 * k + 16],
+                                        dst=T["recv%d" % rnd][:, 16 * r:16 * r + 16]))
+        g.remote_dma_fused(tr, local_sem=T.sem["loc%d" % rnd])
+        count["loc%d" % rnd] = 3 * PER
+        count["arr%d" % rnd] = 3 * PER
+
+    def arrive(rnd):
+        nm = "recv%d" % rnd
+        op("t", lambda e: e.matmul(T.pb7[0:64, 128:256], T[nm][:, 0:64], T.IdF[:], True, True),
+           R=[a(nm), a("IdF")], W=[a("pb7", 128, 256)], extra=[("arr%d" % rnd, 3 * PER)])
+        op("s", lambda e: e.activation(T.Rw[0:64, :], T.pb7[0:64, 128:256], F.Copy), R=[a("pb7", 128, 256)], W=[a("Rw")])
+
+    bounds = [(512 * c, min(512 * c + 512, M)) for c in range(10)]
+    bank1 = ["pb0", "pb1", "pb2", "pb3", "pb4", "pb5", "pb6", "pb0", "pb1", "pb2"]
+    for c, (n0, n1) in enumerate(bounds):
+        G, P = a("G", n0, n1), a(bank1[c], 0, n1 - n0)
+        gtt(G, VW, a("invU", n0 // 16, n1 // 16), a("wrep", n0, n1), A.mult)
+        if c == 1:
+            slots()
+        if c in (4, 5):
+            mm(P, a("IdB"), a("uwin", n0, n1), True, False)
+        if c == 2:
+            for nm in ("x2c", "wc"):
+                op("v", lambda e, nm=nm: e.memset(T[nm][96:128, 448:CB], 0.0), W=[a(nm)])
+            op("v", lambda e: e.memset(T.Rw[64:128, :], 0.0), W=[a("Rw")])
+        if c == 9:
+            sca(a("ADD"), a("shU"), a("Rw"))
+            gat("s", a("D1"), a("ADD"), a("SRu"))
+            mm(FX, a("NegR"), a("D1"), False, True)
+        mm(P, a("NegR"), G, c > 5, True)
+        if c == 1:
+            message()
+            scp(a("send1"), a("pb7", 0, 48))
+            send(1)
+        if c < 6:
+            scp(a("win", n0, n1), P)
+        if c < 4:
+            z0 = MW // 2 + c * H
+            scp(a("ADD", z0, z0 + H), a("uwin", 0, H), F.Copy, 0.0)
+        if c == 6:
+            arrive(1)
+        if c == 7:
+            mm(FX, a("NegR"), a("S1"), True, False)
+        if c > 7:
+            for k in ((6, 7) if c == 8 else (8, 9)):
+                if c == 8:
+                    continue
+                n0, n1 = bounds[k - 2]
+                tt(a("win", n0, n1), a("uwin", n0, n1), a(bank1[k - 2], 0, n1 - n0), A.add)
+    tt(a("win", *bounds[8]), a("uwin", *bounds[8]), a(bank1[8]), A.add)
+    tt(a("x2s"), a("uslot"), FX, A.add)
+    tt(a("win", *bounds[9]), a("uwin", *bounds[9]), a(bank1[9], 0, bounds[9][1] - bounds[9][0]), A.add)
+    for k in range(3):
+        sca(a("win"), a("SRu", 8 * k, 8 * k + 8), a("x2s", 128 * k, 128 * k + 128))
+    for nm, src, sem in (("wc", "wrep", "dwc"), ("x2c", "win", "dx2")):
+        for c in range(8):
+            n = min(CB, M - CB * c)
+            dma("y", sem, lambda e, c=c, n=n, nm=nm, src=src: e.dma_start(
+                T[nm][16 * c:16 * c + 16, 0:n], T[src][16 * c:16 * c + 16, CB * c:CB * c + n]), R=[a(src, 0, M)], W=[a(nm)])
+
+    def perm(lo, hi):
+        for k in range(lo, hi):
+            aa, jj, i4 = k // 4, k // 2 % 2, k % 2
+            s, t = 8 * jj + 2 * aa + i4, 40 * (2 * aa + jj) + i4
+            op("v", lambda e, s=s, t=t: e.tensor_copy(T.invP[:, s:320:16], T.invU[:, t:t + 39:2]),
+               R=[a("invU")], W=[a("invP")], acc=True)
+
+    def compact():
+        ts(a("mk", 4, 5), a("g16", 0, 1), float(CB), A.mult)
+        ts(a("mk", 5, 6), a("g16", 0, 1), 16.0, A.mult)
+        ts(a("c1"), a("SRi"), T.mk[:, 4:5], A.subtract, R=[a("mk", 4, 5)])
+        ts(a("dmp"), a("dmp0"), T.mk[:, 5:6], A.subtract, R=[a("mk", 5, 6)])
+        ts(a("c2"), a("c1"), 0.0, A.is_ge)
+        ts(a("c3"), a("c1"), float(CB), A.is_lt)
+        tt(a("c4"), a("c1"), a("dmp"), A.subtract)
+        tt(a("c2"), a("c2"), a("c3"), A.mult)
+        tt(a("c4"), a("c4"), a("c2"), A.mult)
+        tt(a("c4"), a("c4"), a("dmp"), A.add)
+        cp(a("cpU"), a("c4"))
+
+    cuts = [0, 256, 512] + [512 * k for k in range(2, 8)] + [3840, 4096]
+    for j in range(len(cuts) - 1):
+        x0, x1 = cuts[j], cuts[j + 1]
+        bank = "pb%d" % (0, 1, 2, 4, 5, 6)[j % 6]
+        gat("v" if j == 0 else "s", a("X2", x0, x1), a("win", 0, M), a("connU", x0 // 16, x1 // 16))
+        kmul(bank, "KlF", "X2", x0, x1)
+        if j == 0:
+            perm(0, 8)
+        stmul(bank, x0, x1)
+        if j in (1, 2):
+            perm(4 + 4 * j, 8 + 4 * j)
+        if j == 3:
+            op("v", lambda e: e.transpose(T.wT[:], T.wc[:]), R=[a("wc")], W=[a("wT")])
+        if j == 4:
+            op("v", lambda e: e.transpose(T.xT[:], T.x2c[:]), R=[a("x2c")], W=[a("xT")])
+        if j == 5:
+            compact()
+
+    parts = [(0, 256, "pb0"), (256, 512, "pb1"), (512, 640, "pb2")]
+
+    def finish(k):
+        lo, hi, bank = parts[k]
+        tt(a("yt", lo, hi), a(bank, 0, hi - lo), a("wT", lo, hi), A.mult)
+        tt(a("yu", lo, hi), a("xT", lo, hi), a("yt", lo, hi), A.subtract)
+        op("v", lambda e: e.transpose(T.Y[:, lo:hi], T.yu[:, lo:hi]), R=[a("yu", lo, hi)], W=[a("Y", lo, hi)])
+
+    pieces = [("s", 0), ("v", 512), ("s", 768), ("s", 1280), ("v", 1792), ("s", 2304), ("s", 2816), ("v", 3328), ("s", 3840),
+              ("s", 4352), ("v", 4864)]
+    slots()
+    message()
+    for k, (q, lo) in enumerate(pieces):
+        hi = (pieces + [("", 8 * CB)])[k + 1][1]
+        gat(q, a("G", lo, hi), VW, a("invP", lo // 16, hi // 16))
+        if k == 1:
+            cp(a("send2"), a("pb7", 0, 48))
+            send(2)
+        for b in range(lo // 128, hi // 128):
+            p0, p1, bank = parts[b // 16]
+            o = 16 * b - p0
+            mm(a(bank, o, o + 16), a("G", 128 * b, 128 * b + 128), a("PosR", 0, 16), True, True)
+        if k == 6:
+            mm(FX, a("NegR"), a("S1"), True, False)
+        if k == 8:
+            arrive(2)
+    finish(0)
+    sca(a("ADD"), a("shU"), a("Rw"))
+    gat("s", a("D1"), a("ADD"), a("SRu"))
+    mm(FX, a("NegR"), a("D1"), False, True)
+    finish(1)
+    finish(2)
+    tt(a("x3s"), a("x2s"), FX, A.add)
+    for k in range(3):
+        sca(a("Y"), a("cpU", 8 * k, 8 * k + 8), a("x3s", 128 * k, 128 * k + 128))
+    for c in range(8):
+        n = min(CB, M - CB * c)
+        dma("y" if c % 2 == 0 else "s", "dy",
+            lambda e, c=c, n=n: e.dma_start(T.y[:, CB * c:CB * c + n], T.Y[16 * c:16 * c + 16, 0:n]), R=[a("Y", 0, CB)])
+
+    wait("g", [(name, count[name]) for name in sorted(count)])

@@ -1,5 +1,5 @@
 import numpy as np
-from concourse.bass import DstId, RemoteDMATransfer, IndirectOffsetOnAxis
+from concourse.bass import DstId, RemoteDMATransfer
 from concourse.mybir import dt, AluOpType, AxisListType, ActivationFunctionType
 
 A = AluOpType
@@ -7,26 +7,43 @@ F = ActivationFunctionType
 E, M, CAPP = 4096, 4928, 128
 MW = M + CAPP
 RUN = MW // 16
-NK = M // 16
-ES = 2304
+ES = 2016
+D0 = 384
 CB = 640
-YW = CB + CAPP
+AF = 3160
 PER = 4
+SG = 0
+SD = (SG, 2048, E)
+WD = (0, 1536, 3072, M)
+
+R1 = [512, 512, 256, 256] + [512] * 4 + [256, 256]
+ORDER1 = ("s0 k0 s1 k1 addS lists v2 s3 m0 s4 mask k3 k2 m1 s5 addV m2 m3 invU invF k4 m4 pick k5 m5 u0 u2 mark s6 k6 m6 sum "
+          "s7 u3 k7 s8 k8 keep u1 s9 k9 m7 u5 m8 u6 m9 u4")
+N1 = [256, 256] + [512] * 8 + [320]
+ORDER2 = ("slots v0 k0 message send dumps v1 out k1 consts v2 k2 v3 k3 v4 places k4 e1 e2 mark0 mark1 mark2 v5 k5 e3 v6 u7 k6 "
+          "v7 arrive k7 wslot turn v8 k8 e4 e5 v9 add uslot u8 k9 e6 e7 total v10 sum e8 e9 k10 conn scale slot a10")
+R2 = [128, 128, 256] + [512] * 6 + [256, 256]
+ORDER3 = ("v0 k0 s1 k1 s2 k2 m0 s3 k3 m1 m2 compact s4 k4 m3 mark0 s5 k5 m4 mark1 s6 k6 m5 mark2 s7 k7 m6 s8 k8 order m7 invP "
+          "s9 k9 m8 ylist s10 k10 m9 m10")
+N2 = [512, 256, 512, 512, 512, 512, 512, 512, 512, 512, 256]
+FIN = (0, 224, 416, 544, 640)
+ORDER4 = ("s0 slots v1 send s2 k0 v3 s4 k1 k2 k3 s6 v5 t0 w0 k4 s7 k5 k6 x0 t1 arrive turn w1 add total0 s8 k7 total1 k8 x1 t2 "
+          "total2 s9 s10 k9 k10 w2 sum0 sum1 t3 x2 w3 slot0 slot1 x3 sum2 slot2")
 
 _F = "float32 "
 _B = "bfloat16 "
 _I = "int32 "
 _U = "uint16 "
 _SB = {
-    256: _I + "connI piI " + _U + "connU piU " + _F + "piN piT",
-    MW: _B + "uwin wrep " + _F + "Wv Ws win ADD",
-    E: _B + "strep X1 " + _F + "X2", ES: _F + "dat", E + 8: _F + "V", 8 * CB: _F + "G",
-    NK: _F + "invV invS invT", 320: _U + "invU invP",
-    128: _I + "idm idt asI asJ " + _F + "PosR NegR IdF KlF Rw " + _B + "IdB asB Yb KlB",
-    2: _I + "pI g16 zI", 8: _F + "mk " + _B + "keB " + _I + "shI " + _U + "shU",
-    24: _F + "shM SRf sqN sqT dmp0 dmp c1 c2 c3 c4 " + _I + "SRi sqI " + _U + "SRu piS clU cpU",
-    384: _F + "O1 O2 Om uslot wslot S1 D1 x2s x3s", 48: _F + "send1 send2", 64: _F + "recv1 recv2",
-    CB: _B + "wc wT " + _F + "x2c xT yt yu", YW: _F + "Y",
+    256: _I + "connI piI " + _U + "connU piU " + _F + "piT " + _B + "oneB",
+    MW: _B + "uwin wrep " + _F + "Wv Ws ADD", M + 384: _F + "win",
+    E: _B + "strep srow X1 " + _F + "X2", 6 * D0: _F + "dat", E + 8: _F + "V", 8 * CB: _F + "G",
+    RUN: _F + "zero invV invS invF", 320: _U + "invU invP " + _F + "invG",
+    128: _F + "oneF NegR IdF KlF Bf Rw frow " + _B + "IdB asB Yb KlB",
+    2: _F + "base", 8: _B + "keB " + _I + "shI " + _U + "shU", 20: _F + "m2 " + _U + "pmU",
+    24: _F + "sh3F dmp dmpS c1 c2 c3 " + _I + "sh3 gid low " + _U + "clU cnU cpU", 72: _I + "LI " + _U + "LU",
+    384: _F + "msk O1 O2 rr ids uslot wslot S1 D1 " + _B + "Ab", 48: _F + "send1 send2", 64: _F + "recv1 recv2",
+    CB: _B + "wc " + _F + "x2c", CB + 240: _F + "Wc", CB + 384: _F + "Y", CB // 16: _F + "yF " + _U + "yU",
 }
 SCRATCH = {}
 for _n in _SB:
@@ -39,8 +56,9 @@ for _n in _SB:
 for _k in range(8):
     SCRATCH["pb%d" % _k] = ("psum", [128, 512], "float32")
 
-SEMAPHORES = ["cv", "cs", "ct", "cg", "dconn", "dshare", "dke", "du", "dstr", "dwr", "dxv", "dxs", "dwc", "dx2", "dy",
-              "arr1", "arr2", "loc1", "loc2"]
+SEMAPHORES = ["cv", "cs", "ct", "cg", "dconn", "dshare", "dke", "du", "dWs", "dWv", "dsh", "drow", "ds1", "ds2", "ds3", "ds4",
+              "dw1", "dw2", "dw3", "dw4", "dw5", "dw6", "dxv", "dxs", "dwc", "dx2", "dc1", "dc2", "dc3",
+              "dy", "arr1", "arr2", "loc1", "loc2"]
 
 
 def rank_program(g, core, T, topo):
@@ -75,7 +93,7 @@ def rank_program(g, core, T, topo):
                         hit = True
                     else:
                         hit = l2 < hi and lo < h2 and (w2 or wr)
-                        if same and (not w2 or (wr and acc)):
+                        if same and wr and acc:
                             hit = False
                     if hit:
                         toks.append((sem, count[sem] if sem[:1] == "d" else val))
@@ -98,41 +116,41 @@ def rank_program(g, core, T, topo):
         count[sem] = count.get(sem, 0) + 1
         record(q, R, W, sem, count[sem])
 
-    def dma(q, sem, fn, R=(), W=()):
+    def dma(q, sem, out, in_, R=(), W=()):
         wait(q, needs(q, R, W, sem, False))
-        fn(queue[q]).then_inc(T.sem[sem], 16)
+        queue[q].dma_start(out, in_).then_inc(T.sem[sem], 16)
         count[sem] = count.get(sem, 0) + 16
         record(q, R, W, sem, count[sem])
 
     def a(name, lo=0, hi=None):
         return (name, lo, SCRATCH[name][1][1] if hi is None else hi)
 
-    def ap(x):
-        return T[x[0]][:, x[1]:x[2]]
+    def ap(x, P=128):
+        return T[x[0]][0:P, x[1]:x[2]]
 
     def fill(x, val):
         op("v", lambda e: e.memset(ap(x), val), W=[x])
 
-    def ts(out, in0, s1, op0, s2=None, op1=None, R=()):
+    def ts(out, in0, s1, op0, s2=None, op1=None, R=(), P=128):
         if op1 is None:
-            op("v", lambda e: e.tensor_scalar(ap(out), ap(in0), s1, None, op0), R=[in0] + list(R), W=[out])
+            op("v", lambda e: e.tensor_scalar(ap(out, P), ap(in0, P), s1, None, op0), R=[in0] + list(R), W=[out])
         else:
-            op("v", lambda e: e.tensor_scalar(ap(out), ap(in0), s1, s2, op0, op1), R=[in0] + list(R), W=[out])
+            op("v", lambda e: e.tensor_scalar(ap(out, P), ap(in0, P), s1, s2, op0, op1), R=[in0] + list(R), W=[out])
 
-    def tt(out, in0, in1, o):
-        op("v", lambda e: e.tensor_tensor(ap(out), ap(in0), ap(in1), o), R=[in0, in1], W=[out])
+    def tt(out, in0, in1, o, P=128):
+        op("v", lambda e: e.tensor_tensor(ap(out, P), ap(in0, P), ap(in1, P), o), R=[in0, in1], W=[out])
 
-    def cp(out, in_):
-        op("v", lambda e: e.tensor_copy(ap(out), ap(in_)), R=[in_], W=[out])
+    def cp(out, in_, P=128):
+        op("v", lambda e: e.tensor_copy(ap(out, P), ap(in_, P)), R=[in_], W=[out])
 
-    def scp(out, in_, func=F.Copy, scale=1.0):
-        op("s", lambda e: e.activation(ap(out), ap(in_), func, scale=scale), R=[in_], W=[out])
+    def scp(out, in_, scale=1.0, P=128):
+        op("s", lambda e: e.activation(ap(out, P), ap(in_, P), F.Copy, scale=scale), R=[in_], W=[out])
 
-    def gat(q, out, win, off):
+    def gat(q, out, win, off, scale=1.0):
         if q == "v":
             op("v", lambda e: e.tensor_copy(ap(out), ap(win).indirect(ap(off))), R=[win, off], W=[out])
         else:
-            op("s", lambda e: e.activation(ap(out), ap(win).indirect(ap(off)), F.Copy), R=[win, off], W=[out])
+            op("s", lambda e: e.activation(ap(out), ap(win).indirect(ap(off)), F.Copy, scale=scale), R=[win, off], W=[out])
 
     def gtt(out, win, off, in1, o):
         op("v", lambda e: e.tensor_tensor(ap(out), ap(win).indirect(ap(off)), ap(in1), o), R=[win, off, in1], W=[out])
@@ -140,161 +158,210 @@ def rank_program(g, core, T, topo):
     def sca(win, off, in_):
         op("v", lambda e: e.tensor_copy(ap(win).indirect(ap(off)), ap(in_)), R=[off, in_], W=[win])
 
-    def mm(out, lhsT, rhs, start, stop):
-        op("t", lambda e: e.matmul(ap(out), ap(lhsT), ap(rhs), start, stop), R=[lhsT, rhs], W=[out], acc=not start)
+    def silu_sca(win, off, in_):
+        op("s", lambda e: e.activation(ap(win).indirect(ap(off)), ap(in_), F.Silu), R=[off, in_], W=[win])
 
-    def iota(out, pattern, base, cm, imprecise=False):
-        if imprecise:
-            op("g", lambda e: e.iota(ap(out), pattern, base, cm, allow_small_or_imprecise_dtypes=True), W=[out])
+    def mm(out, lhsT, rhs, start=True, stop=True, K=128, P=128, extra=()):
+        op("t", lambda e: e.matmul(ap(out, P), ap(lhsT, K), ap(rhs, K), start, stop), R=[lhsT, rhs], W=[out], acc=not start,
+           extra=extra)
+
+    moved = [False]
+
+    def gop(fn, R, W, shift):
+        op("g", fn, R=R, W=W, extra=[("cg", count.get("cg", 0))] if shift or moved[0] else [])
+        moved[0] = shift
+
+    def iota(out, pattern, base, cm, p0=0, p1=128):
+        gop(lambda e: e.iota(T[out[0]][p0:p1, out[1]:out[2]], pattern, base, cm, allow_small_or_imprecise_dtypes=True),
+            [], [out], p0 > 0)
+
+    def select(out, in_, pattern, cmp, base, cm, P=128, p0=0, other=0.0):
+        gop(lambda e: e.affine_select(T[out[0]][p0:p0 + P, out[1]:out[2]], T[in_[0]][p0:p0 + P, in_[1]:in_[2]], pattern, cmp,
+                                      other, base, cm), [in_], [out], p0 > 0)
+
+    def run(order, step):
+        for w in order.split():
+            name = w.rstrip("0123456789")
+            if name == w:
+                step[w]()
+            else:
+                step[name](int(w[len(name):]))
+
+    def cuts(widths):
+        c = [0]
+        for n in widths:
+            c.append(c[-1] + n)
+        return c
+
+    def spread(q, sem, step, nm, row, lo, hi):
+        x = a(nm, lo, hi)
+        if step == 0:
+            for p in range(0, 128, 32):
+                dma(q, sem, T[nm][p:p + 1, lo:hi], T[row][0:1, lo:hi], W=[x])
         else:
-            op("g", lambda e: e.iota(ap(out), pattern, base, cm), W=[out])
+            d, n = ((32, 8), (4, 4))[step - 1]
+            for m in range(1, n):
+                dma(q, sem, T[nm][m * d // n:128:d, lo:hi], T[nm][0:128:d, lo:hi], R=[x], W=[x])
 
-    def broadcast(sem, out, row):
-        dma("g", sem, lambda e: e.indirect_dma_start(ap(out), None, T[row][:], IndirectOffsetOnAxis(ap=T.zI[:, 0:1], axis=0),
-                                                     bounds_check=0), R=[a("zI")], W=[out])
-
-    dma("y", "dconn", lambda e: e.dma_start(T.connI[:], T.conn[:]), W=[a("connI")])
-    dma("y", "dshare", lambda e: e.dma_start(T.shI[:], T.share[:]), W=[a("shI")])
-    dma("y", "dke", lambda e: e.dma_start(T.keB[0:8, :], T.ke[:]), W=[a("keB")])
-    for c in range(8):
-        dma("y", "du", lambda e, c=c: e.dma_start(T.uwin[16 * c:16 * c + 16, 0:M], T.u[:]), W=[a("uwin", 0, M)])
-
-    H, W3, S3 = 632, 3 * (MW // 4), MW - 632
-    fill(a("Wv", 0, H), 0.0)
-    fill(a("zI"), 0)
-    iota(a("dat", 0, 1024), [[-1, 1024]], E, 0, True)
-    iota(a("Wv", W3, MW), [[0, MW - W3]], 0, 0, True)
-    iota(a("Ws", S3, MW), [[0, MW - S3]], 0, 0, True)
-    iota(a("dat", 1024, 2048), [[-1, 1024]], E - 1024, 0, True)
-    broadcast("dstr", a("strep"), "st")
-    iota(a("idm"), [[-1, 128]], 128, 1)
-    iota(a("pI"), [[0, 2]], 0, 1)
-    op("g", lambda e: e.iota(T.asI[0:8, :], [[1, 128]], 128, -16), W=[a("asI")])
-    iota(a("dmp0"), [[0, 3], [16, 8]], CB, 1, True)
-    iota(a("dat", 2048, ES), [[-1, ES - 2048]], E - 2048, 0, True)
-    broadcast("dwr", a("wrep", 0, M), "w")
-    iota(a("ADD", 0, MW // 2), [[0, MW // 2]], 0, 0, True)
-
-    scp(a("Ws", 0, H), a("Wv", 0, H), F.Silu)
-    for lo, hi in ((H, 2 * H), (2 * H, 4 * H), (4 * H, S3)):
-        scp(a("Ws", lo, hi), a("Ws", 0, hi - lo), F.Silu)
-    fill(a("Wv", H, 4 * H), 0.0)
-
-    def runs(out, src, i_, n_, t_):
-        ts(i_, src, 15, A.bitwise_and)
-        ts(n_, src, 1.0 / (16 * RUN - 1), A.mult)
-        tt(t_, n_, i_, A.add)
-        ts(out, t_, (16 * RUN - 1) / 16.0, A.mult, 0.25, A.add)
-
-    runs(a("piU"), a("connI"), a("piI"), a("piN"), a("piT"))
-    fill(a("Wv", 4 * H, W3), 0.0)
-
-    def scat_s(e0, e1):
-        off, x = a("piU", e0 // 16, e1 // 16), a("dat", e0, e1)
-        op("s", lambda e: e.activation(ap(a("Ws")).indirect(ap(off)), ap(x), F.Silu), R=[off, x], W=[a("Ws")])
-
-    def scat_v(e0, e1):
-        off, x = a("piU", e0 // 16, e1 // 16), a("dat", e0 - ES, e1 - ES)
-        op("v", lambda e: e.tensor_scalar(ap(a("Wv")).indirect(ap(off)), ap(x), 1.0, float(-ES), A.mult, A.add),
-           R=[off, x], W=[a("Wv")])
-
-    scat_s(0, 1024)
-    scat_v(ES, ES + 1024)
-    scat_s(1024, 2048)
-    scat_v(ES + 1024, E)
-    scat_s(2048, ES)
-    for nm, wn, sem in (("invV", "Wv", "dxv"), ("invS", "Ws", "dxs")):
-        for i in range(16):
-            dma("y", sem, lambda e, i=i, nm=nm, wn=wn: e.dma_start(T[nm][i:128:16, :], T[wn][i:128:16, RUN * i:RUN * i + NK]),
-                R=[a(wn)], W=[a(nm)])
-
-    cp(a("connU"), a("connI"))
-    op("v", lambda e: e.tensor_scalar(T.asJ[0:8, :], T.asI[0:8, :], 4, None, A.arith_shift_right), R=[a("asI")], W=[a("asJ")])
-    ts(a("idt"), a("idm"), 15, A.bitwise_and)
-    op("v", lambda e: e.tensor_scalar(T.asB[0:8, :], T.asJ[0:8, :], 8, None, A.is_equal), R=[a("asJ")], W=[a("asB")])
-    op("t", lambda e: e.matmul(T.pb1[0:8, 0:128], T.keB[0:8, 0:8], T.asB[0:8, :], True, True),
-       R=[a("keB"), a("asB")], W=[a("pb1", 0, 128)])
-    ts(a("PosR"), a("idt"), 0, A.is_equal)
-    ts(a("g16"), a("pI"), 4, A.arith_shift_right)
-    op("v", lambda e: e.tensor_copy(T.Yb[0:8, :], T.pb1[0:8, 0:128]), R=[a("pb1", 0, 128)], W=[a("Yb")])
-    op("t", lambda e: e.matmul(T.pb2[:, 0:128], T.asB[0:8, :], T.Yb[0:8, :], True, True),
-       R=[a("asB"), a("Yb")], W=[a("pb2", 0, 128)])
+    dma("y", "dconn", T.connI[:], T.conn[:], W=[a("connI")])
+    dma("y", "dke", T.keB[0:8, :], T.ke[:], W=[a("keB")])
+    if SG:
+        dma("s", "drow", T.srow[0:1, 0:SG], T.st[0:1, 0:SG], W=[a("srow")])
+    spread("s", "ds1", 0, "strep", "st", SG, E)
+    fill(a("zero"), 0.0)
+    for wn in ("Ws", "Wv"):
+        dma("s", "d" + wn, T[wn][0:128:16, :], T.zero[:], R=[a("zero")], W=[a(wn)])
     for k, q in enumerate(partners):
-        ts(a("mk", k, k + 1), a("g16", 0, 1), q, A.is_equal)
-    tt(a("KlB"), a("pb2", 0, 128), a("PosR"), A.mult)
+        dma("y", "dshare", T.sh3[0:16, 8 * k:8 * k + 8], T.share[16 * q:16 * q + 16, :], W=[a("sh3")])
+    spread("y", "dw1", 0, "wrep", "w", 0, M)
+    for c in range(8):
+        dma("y", "du", T.uwin[16 * c:16 * c + 16, 0:M], T.u[:], W=[a("uwin", 0, M)])
+    spread("y", "ds2", 1, "strep", "st", SG, E)
+    spread("y", "dw2", 1, "wrep", "w", WD[0], WD[1])
+    dma("y", "dsh", T.shI[:], T.share[:], W=[a("shI")])
+    spread("y", "ds3", 2, "strep", "st", SD[0], SD[1])
+
+    iota(a("dat", 0, D0), [[-1, D0]], E, 0)
+    fill(a("oneB"), 1.0)
+    fill(a("oneF"), 1.0)
+    select(a("Ab", 0, 128), a("oneB", 0, 128), [[0, 8], [-1, 16]], A.is_equal, 0, 1, P=16)
+    select(a("asB"), a("oneB", 0, 128), [[-1, 8], [0, 16]], A.is_equal, 0, 1, P=8)
+    iota(a("frow"), [[0, 8], [40, 8], [1, 2]], 0, 0, 0, 1)
+    iota(a("m2"), [[2, 20]], 0, 0, 0, 1)
+    for x0 in range(0, SG, 512):
+        gop(lambda e: e.partition_broadcast(T.strep[:, x0:x0 + 512], T.srow[0:1, x0:x0 + 512], 128), [a("srow")],
+            [a("strep", x0, x0 + 512)], True)
+    select(a("IdF"), a("oneF"), [[-1, 128]], A.is_equal, 0, 1)
+    select(a("IdB"), a("oneB", 0, 128), [[-1, 128]], A.is_equal, 0, 1)
+    select(a("Ab", 128, 384), a("oneB"), [[0, 16], [-1, 16]], A.is_equal, 0, 1, P=16)
+    select(a("Bf"), a("oneF"), [[-16, 8], [0, 16]], A.is_ge, 0, 1)
+    select(a("Bf"), a("Bf"), [[16, 8], [0, 16]], A.is_ge, 15, -1)
+    iota(a("rr"), [[0, 24], [32767, 16]], 0, 0)
+    for z in (a("V", E, E + 8), a("recv1", 16 * r, 16 * r + 16), a("recv2", 16 * r, 16 * r + 16), a("uwin", M, MW),
+              a("wrep", M, MW)):
+        iota(z, [[0, z[2] - z[1]]], 0, 0)
+    iota(a("ids"), [[1, 384]], M, 0)
+    iota(a("dmpS"), [[0, 3], [16, 8]], E, 1)
+    iota(a("Rw"), [[0, 128]], 0, 0, 64, 128)
+
+    def fill_add(lo, hi):
+        for x0 in range(lo, hi, 632):
+            iota(a("ADD", x0, x0 + 632), [[0, 632]], 0, 0)
+
+    fill_add(0, AF)
+    ts(a("dat", D0, 2 * D0), a("dat", 0, D0), float(-D0), A.add)
+    ts(a("dat", 2 * D0, 4 * D0), a("dat", 0, 2 * D0), float(-2 * D0), A.add)
+    for k in (4, 5):
+        x, y = a("dat", k * D0, k * D0 + D0), a("dat", 0, D0)
+        op("s", lambda e, x=x, y=y, k=k: e.activation(ap(x), ap(y), F.Silu, bias=float(-k * D0)), R=[y], W=[x])
+    mm(a("pb0", 0, 128), a("Ab", 0, 128), a("Ab", 0, 128), K=16)
+    ts(a("NegR"), a("pb0", 0, 128), -1.0, A.mult)
+
+    def runs(k, lo, hi):
+        if k == 0:
+            ts(a("piI", lo, hi), a("connI", lo, hi), 15, A.bitwise_and)
+            ts(a("pb6", lo, hi), a("connI", lo, hi), 1.0 / (16 * RUN - 1), A.mult)
+        elif k == 1:
+            tt(a("piT", lo, hi), a("pb6", lo, hi), a("piI", lo, hi), A.add)
+        else:
+            ts(a("piU", lo, hi), a("piT", lo, hi), (16 * RUN - 1) / 16.0, A.mult, 0.25, A.add)
+
     for k in range(3):
-        ts(a("shM", 8 * k, 8 * k + 8), a("shI"), T.mk[:, k:k + 1], A.mult, R=[a("mk", k, k + 1)])
-    mm(a("pb0", 0, 24), a("PosR"), a("shM"), True, True)
-    fill(a("uwin", M, MW), 0.0)
-    fill(a("wrep", M, MW), 0.0)
-    ts(a("IdF"), a("idm"), 128, A.is_equal)
-    cp(a("SRi"), a("pb0", 0, 24))
-    cp(a("SRu"), a("pb0", 0, 24))
-    runs(a("piS"), a("SRi"), a("sqI"), a("sqN"), a("sqT"))
+        runs(k, 0, ES // 16)
+    mm(a("pb1", 0, 128), a("keB"), a("asB"), K=8, P=8)
+    ts(a("Yb"), a("pb1", 0, 128), -1.0, A.mult, P=8)
+    mm(a("pb2", 0, 128), a("asB"), a("Yb"), K=8)
+    runs(0, ES // 16, E // 16)
+    cp(a("sh3F"), a("sh3"), P=16)
+    runs(1, ES // 16, E // 16)
+    cp(a("connU"), a("connI"))
+    runs(2, ES // 16, E // 16)
+    tt(a("KlB"), a("pb2", 0, 128), a("NegR"), A.mult)
 
-    gat("v", a("O1"), a("Wv"), a("piS"))
-    gtt(a("O2"), a("Ws"), a("piS"), a("O1"), A.add)
-    for k in range(3):
-        tt(a("Om", 128 * k, 128 * k + 128), a("O2", 128 * k, 128 * k + 128), a("PosR"), A.mult)
+    silu_sca(a("Ws"), a("piU", 0, ES // 16), a("dat", 0, ES))
+    off, x = a("piU", ES // 16, E // 16), a("dat", 0, E - ES)
+    op("v", lambda e: e.tensor_scalar(ap(a("Wv")).indirect(ap(off)), ap(x), 1.0, float(-ES), A.mult, A.add),
+       R=[off, x], W=[a("Wv")])
+    dma("y", "dxs", T.invS[:], T.Ws[0:128:16, :], R=[a("Ws")], W=[a("invS")])
+    dma("y", "dxv", T.invV[:], T.Wv[0:128:16, :], R=[a("Wv")], W=[a("invV")])
+    spread("y", "dw3", 1, "wrep", "w", WD[1], M)
+    spread("y", "ds4", 2, "strep", "st", SD[1], SD[2])
+    for k in range(len(WD) - 1):
+        spread("y", "dw%d" % (4 + k), 2, "wrep", "w", WD[k], WD[k + 1])
 
-    def comp_lists(i0, i1):
-        for i in range(i0, i1):
-            op("t", lambda e, i=i: e.matmul(T.pb3[:, 0:24], T.IdF[:], T.Om[:, i:384:16], i == 0, i == 15),
-               R=[a("IdF"), a("Om")], W=[a("pb3", 0, 24)], acc=i > 0)
+    mm(a("pb3", 0, 24), a("NegR"), a("sh3F"), K=16)
+    mm(a("pb3", 32, 52), a("frow"), a("oneF", 0, 20), True, False, K=1)
+    mm(a("pb3", 32, 52), a("oneF"), a("m2"), False, True, K=1)
+    SR = [a("LU", 8 * k, 8 * k + 8) for k in range(3)]
 
-    def kmul(bank, K, X, x0, x1):
-        mm(a(bank, 0, x1 - x0), a(K), a(X, x0, x1), True, True)
+    def lists():
+        ts(a("LI", 0, 24), a("pb3", 0, 24), -1.0, A.mult)
+        ts(a("pmU"), a("pb3", 32, 52), float(M // 16), A.min, 0.25, A.add)
+        ts(a("LI", 24, 48), a("LI", 0, 24), 4, A.arith_shift_right)
+        ts(a("LI", 48, 72), a("LI", 0, 24), 15, A.bitwise_and)
+        cp(a("shU"), a("shI"))
+        cp(a("LU"), a("LI"))
 
-    def stmul(bank, x0, x1):
-        tt(a("V", x0, x1), a(bank, 0, x1 - x0), a("strep", x0, x1), A.mult)
+    def dumps():
+        scp(a("dmpS"), a("dmpS"), 16.0 / (E - 1))
 
-    for j in range(8):
-        x0, x1 = 512 * j, 512 * j + 512
-        bank = "pb%d" % (4 + j % 4)
-        gat("s", a("X1", x0, x1), a("uwin"), a("connU", 32 * j, 32 * j + 32))
-        kmul(bank, "KlB", "X1", x0, x1)
-        stmul(bank, x0, x1)
-        if j == 0:
-            tt(a("KlF"), a("pb2", 0, 128), a("PosR"), A.mult)
-            ts(a("IdB"), a("idm"), 128, A.is_equal)
-        if 1 <= j <= 4:
-            comp_lists(4 * j - 4, 4 * j)
-        if j == 1:
-            ts(a("NegR"), a("idt"), 0, A.is_equal, -1.0, A.mult)
-            fill(a("V", E, E + 8), 0.0)
-        if j == 2:
-            cp(a("shU"), a("shI"))
-            for k in (1, 2):
-                fill(a("recv%d" % k, 16 * r, 16 * r + 16), 0.0)
-        if j == 4:
-            tt(a("invT"), a("invV"), a("invS"), A.add)
-        if j == 5:
-            ts(a("invU", 0, NK), a("invT"), -1.0, A.mult, E + 0.25, A.add)
-            fill(a("invU", NK, 320), E)
-        if j == 6:
-            ts(a("clU"), a("pb3", 0, 24), -1.0, A.mult, E + 0.25, A.add)
-            for c in range(4):
-                mm(a("pb%d" % c), a("IdB"), a("uwin", 512 * c, 512 * c + 512), True, False)
-    gat("s", a("wslot"), a("wrep"), a("SRu"))
-    gat("s", a("uslot"), a("uwin"), a("SRu"))
+    IV = a("pb7", 0, RUN)
+    CL = a("pb7", 0, 384)
+
+    def uadd(c):
+        n0, n1 = 512 * c, min(512 * c + 512, M)
+        mm(a("pb%d" % (c % 7), 0, n1 - n0), a("IdB"), a("uwin", n0, n1), True, False)
+
+    def keep():
+        op("v", lambda e: e.tensor_tensor_scan(ap(a("O2")), ap(a("rr")), ap(CL), 0.0, A.min, A.max),
+           R=[a("rr"), CL], W=[a("O2")])
+        op("v", lambda e: e.tensor_scalar(ap(a("clU")), T.O2[:, 15:384:16], -16384.0, 16384 + E + 0.25, A.mult, A.add),
+           R=[a("O2")], W=[a("clU")])
+
+    def elements(widths, X, win, lst, K, banks):
+        c = cuts(widths)
+
+        def bank(j):
+            return a("pb%d" % banks[j % len(banks)], 0, widths[j])
+        return {
+            "s": lambda j: gat("s", a(X, c[j], c[j + 1]), win, a(lst, c[j] // 16, c[j + 1] // 16)),
+            "v": lambda j: gat("v", a(X, c[j], c[j + 1]), win, a(lst, c[j] // 16, c[j + 1] // 16)),
+            "k": lambda j: mm(bank(j), a(K), a(X, c[j], c[j + 1])),
+            "m": lambda j: tt(a("V", c[j], c[j + 1]), bank(j), a("strep", c[j], c[j + 1]), A.mult),
+        }
+
+    step = elements(R1, "X1", a("uwin", 0, M), "connU", "KlB", (4, 5, 6))
+    step.update({
+        "u": uadd,
+        "lists": lists,
+        "mask": lambda: gat("s", a("msk"), a("NegR", 0, 16), a("LU", 48, 72), -1.0 / 16384),
+        "addS": lambda: mm(IV, a("IdF"), a("invS"), True, False),
+        "addV": lambda: mm(IV, a("IdF"), a("invV"), False, True),
+        "invU": lambda: ts(a("invU", 0, RUN), IV, -1.0, A.mult, E + 0.25, A.add),
+        "invF": lambda: scp(a("invF"), IV),
+        "pick": lambda: gtt(a("O1"), a("invF"), a("LU", 24, 48), a("msk"), A.mult),
+        "mark": lambda: mm(CL, a("Ab", 0, 128), a("Ab"), True, False, K=16),
+        "sum": lambda: mm(CL, a("Bf"), a("O1"), False, True),
+        "keep": keep,
+    })
+    run(ORDER1, step)
 
     VW = a("V")
-    FX = a("pb3", 0, 384)
     used, masks = [], {}
     for q in sorted(partners, key=lambda q: len(topo.engines(core, T.cores[q]))):
         ok = [e for e in topo.engines(core, T.cores[q]) if e not in used][:PER]
         used += ok
         masks[q] = sum(1 << e for e in ok)
 
-    def slots():
-        gtt(a("S1"), VW, a("clU"), a("wslot"), A.mult)
+    def part(nm, k):
+        return a(nm, 128 * k, 128 * k + 128)
 
-    def message():
-        for k in range(3):
-            mm(a("pb7", 16 * k, 16 * k + 16), a("S1", 128 * k, 128 * k + 128), a("PosR", 0, 16), True, True)
+    def message(k):
+        mm(a("pb7", 16 * k, 16 * k + 16), part("S1", k), a("NegR", 0, 16))
 
-    def send(rnd):
+    def send(rnd, copy):
         nm = "send%d" % rnd
+        copy(a(nm), a("pb7", 0, 48))
         wait("g", needs("g", [a(nm)], [], "loc%d" % rnd, False))
         tr = []
         for k, q in enumerate(partners):
@@ -307,135 +374,172 @@ def rank_program(g, core, T, topo):
         count["arr%d" % rnd] = 3 * PER
 
     def arrive(rnd):
-        nm = "recv%d" % rnd
-        op("t", lambda e: e.matmul(T.pb7[0:64, 128:256], T[nm][:, 0:64], T.IdF[:], True, True),
-           R=[a(nm), a("IdF")], W=[a("pb7", 128, 256)], extra=[("arr%d" % rnd, 3 * PER)])
-        op("s", lambda e: e.activation(T.Rw[0:64, :], T.pb7[0:64, 128:256], F.Copy), R=[a("pb7", 128, 256)], W=[a("Rw")])
+        mm(a("pb7", 128, 256), a("recv%d" % rnd), a("IdF"), P=64, extra=[("arr%d" % rnd, 3 * PER)])
 
-    bounds = [(512 * c, min(512 * c + 512, M)) for c in range(10)]
-    bank1 = ["pb0", "pb1", "pb2", "pb3", "pb4", "pb5", "pb6", "pb0", "pb1", "pb2"]
-    for c, (n0, n1) in enumerate(bounds):
-        G, P = a("G", n0, n1), a(bank1[c], 0, n1 - n0)
-        gtt(G, VW, a("invU", n0 // 16, n1 // 16), a("wrep", n0, n1), A.mult)
-        if c == 1:
-            slots()
-        if c in (4, 5):
-            mm(P, a("IdB"), a("uwin", n0, n1), True, False)
-        if c == 2:
-            for nm in ("x2c", "wc"):
-                op("v", lambda e, nm=nm: e.memset(T[nm][96:128, 448:CB], 0.0), W=[a(nm)])
-            op("v", lambda e: e.memset(T.Rw[64:128, :], 0.0), W=[a("Rw")])
-        if c == 9:
-            sca(a("ADD"), a("shU"), a("Rw"))
-            gat("s", a("D1"), a("ADD"), a("SRu"))
-            mm(FX, a("NegR"), a("D1"), False, True)
-        mm(P, a("NegR"), G, c > 5, True)
-        if c == 1:
-            message()
-            scp(a("send1"), a("pb7", 0, 48))
-            send(1)
-        if c < 6:
-            scp(a("win", n0, n1), P)
-        if c < 4:
-            z0 = MW // 2 + c * H
-            scp(a("ADD", z0, z0 + H), a("uwin", 0, H), F.Copy, 0.0)
-        if c == 6:
-            arrive(1)
-        if c == 7:
-            mm(FX, a("NegR"), a("S1"), True, False)
-        if c > 7:
-            for k in ((6, 7) if c == 8 else (8, 9)):
-                if c == 8:
-                    continue
-                n0, n1 = bounds[k - 2]
-                tt(a("win", n0, n1), a("uwin", n0, n1), a(bank1[k - 2], 0, n1 - n0), A.add)
-    tt(a("win", *bounds[8]), a("uwin", *bounds[8]), a(bank1[8]), A.add)
-    tt(a("x2s"), a("uslot"), FX, A.add)
-    tt(a("win", *bounds[9]), a("uwin", *bounds[9]), a(bank1[9], 0, bounds[9][1] - bounds[9][0]), A.add)
-    for k in range(3):
-        sca(a("win"), a("SRu", 8 * k, 8 * k + 8), a("x2s", 128 * k, 128 * k + 128))
-    for nm, src, sem in (("wc", "wrep", "dwc"), ("x2c", "win", "dx2")):
+    def total(k):
+        gtt(part("D1", k), a("ADD"), SR[k], part("S1", k), A.subtract)
+
+    def place(c):
+        return CB * (4 * (c % 2) + c // 2)
+
+    def compact_copy(nm, src, sem):
         for c in range(8):
-            n = min(CB, M - CB * c)
-            dma("y", sem, lambda e, c=c, n=n, nm=nm, src=src: e.dma_start(
-                T[nm][16 * c:16 * c + 16, 0:n], T[src][16 * c:16 * c + 16, CB * c:CB * c + n]), R=[a(src, 0, M)], W=[a(nm)])
+            n0 = place(c)
+            n = min(CB, M - n0)
+            dma("y", sem, T[nm][16 * c:16 * c + 16, 0:n], T[src][16 * c:16 * c + 16, n0:n0 + n], R=[a(src, 0, M)], W=[a(nm)])
 
-    def perm(lo, hi):
-        for k in range(lo, hi):
-            aa, jj, i4 = k // 4, k // 2 % 2, k % 2
-            s, t = 8 * jj + 2 * aa + i4, 40 * (2 * aa + jj) + i4
-            op("v", lambda e, s=s, t=t: e.tensor_copy(T.invP[:, s:320:16], T.invU[:, t:t + 39:2]),
-               R=[a("invU")], W=[a("invP")], acc=True)
+    def consts():
+        fill_add(AF, MW)
+        iota(a("dmp"), [[0, 3], [16, 8]], CB, 1)
+        iota(a("Wc", 0, CB), [[1, 16], [16, CB // 16]], 0, 0)
+        for k in range(4):
+            iota(a("base"), [[0, 2]], place(2 * k + 1) // 16, 0, 32 * k, 32 * k + 32)
+            select(a("base"), a("base"), [[0, 2]], A.is_ge, -16, 1, 32, 32 * k, float(place(2 * k) // 16))
+        for nm in ("wc", "x2c"):
+            iota(a(nm, 448, CB), [[0, CB - 448]], 0, 0, 96, 128)
+
+    def conn_out():
+        cp(a("piT"), a("connI"))
+        dma("y", "dc1", T.Ws[0:128:16, 0:E], T.piT[:], R=[a("piT")], W=[a("Ws")])
+
+    def conn_places():
+        last = T.O2[:, 15:384:16]
+
+        def from_last(out, s1, s2):
+            op("v", lambda e: e.tensor_scalar(ap(out), last, s1, s2, A.mult, A.add), R=[a("O2")], W=[out])
+        from_last(a("gid"), -16384.0, 16384.0 + E)
+        from_last(a("c1"), -16384.0 / (E - 1), (16384.0 + E) / (E - 1))
+        from_last(a("c2"), -2.0 ** 20, 2.0 ** 20 + 64)
+        ts(a("low"), a("gid"), 15, A.bitwise_and)
+        tt(a("c2"), a("c2"), a("dmpS"), A.min)
+        tt(a("c1"), a("c1"), a("low"), A.add)
+        tt(a("c3"), a("c1"), a("c2"), A.max)
+        ts(a("cnU"), a("c3"), (E - 1) / 16.0, A.mult, 0.25, A.add)
+
+    def conn_mark(k):
+        silu_sca(a("Ws"), a("cnU", 8 * k, 8 * k + 8), part("ids", k))
+        if k == 2:
+            dma("y", "dc2", T.piT[:], T.Ws[0:128:16, 0:E], R=[a("Ws")], W=[a("piT")])
 
     def compact():
-        ts(a("mk", 4, 5), a("g16", 0, 1), float(CB), A.mult)
-        ts(a("mk", 5, 6), a("g16", 0, 1), 16.0, A.mult)
-        ts(a("c1"), a("SRi"), T.mk[:, 4:5], A.subtract, R=[a("mk", 4, 5)])
-        ts(a("dmp"), a("dmp0"), T.mk[:, 5:6], A.subtract, R=[a("mk", 5, 6)])
-        ts(a("c2"), a("c1"), 0.0, A.is_ge)
-        ts(a("c3"), a("c1"), float(CB), A.is_lt)
-        tt(a("c4"), a("c1"), a("dmp"), A.subtract)
-        tt(a("c2"), a("c2"), a("c3"), A.mult)
-        tt(a("c4"), a("c4"), a("c2"), A.mult)
-        tt(a("c4"), a("c4"), a("dmp"), A.add)
-        cp(a("cpU"), a("c4"))
+        b = T.base[:, 0:1]
+        ts(a("gid"), a("LI", 0, 24), 1.0 / CB, A.mult, -0.4992, A.add)
+        ts(a("c1"), a("LI", 48, 72), float(CB // 16), A.mult, b, A.subtract, R=[a("base")])
+        tt(a("c3"), a("LI", 24, 48), a("dmp"), A.subtract)
+        ts(a("c2"), a("gid"), float(CB // 16), A.mult, b, A.is_equal, R=[a("base")])
+        tt(a("c1"), a("c1"), a("c3"), A.add)
+        tt(a("c1"), a("c1"), a("c2"), A.mult)
+        tt(a("c1"), a("c1"), a("dmp"), A.add)
+        cp(a("cpU"), a("c1"))
 
-    cuts = [0, 256, 512] + [512 * k for k in range(2, 8)] + [3840, 4096]
-    for j in range(len(cuts) - 1):
-        x0, x1 = cuts[j], cuts[j + 1]
-        bank = "pb%d" % (0, 1, 2, 4, 5, 6)[j % 6]
-        gat("v" if j == 0 else "s", a("X2", x0, x1), a("win", 0, M), a("connU", x0 // 16, x1 // 16))
-        kmul(bank, "KlF", "X2", x0, x1)
-        if j == 0:
-            perm(0, 8)
-        stmul(bank, x0, x1)
-        if j in (1, 2):
-            perm(4 + 4 * j, 8 + 4 * j)
-        if j == 3:
-            op("v", lambda e: e.transpose(T.wT[:], T.wc[:]), R=[a("wc")], W=[a("wT")])
-        if j == 4:
-            op("v", lambda e: e.transpose(T.xT[:], T.x2c[:]), R=[a("x2c")], W=[a("xT")])
-        if j == 5:
-            compact()
+    def y_mark(k):
+        off, x = a("cpU", 8 * k, 8 * k + 8), part("ids", k)
+        op("v", lambda e: e.tensor_scalar(ap(a("Wc")).indirect(ap(off)), ap(x), 1.0, float(CB - M), A.mult, A.add),
+           R=[off, x], W=[a("Wc")])
+        if k == 2:
+            dma("y", "dc3", T.yF[:], T.Wc[0:128:16, 0:CB], R=[a("Wc")], W=[a("yF")])
 
-    parts = [(0, 256, "pb0"), (256, 512, "pb1"), (512, 640, "pb2")]
+    c1 = cuts(N1)
+    opened = set(w for w in (ORDER1 + " " + ORDER2).split() if w[0] == "u")
 
-    def finish(k):
-        lo, hi, bank = parts[k]
-        tt(a("yt", lo, hi), a(bank, 0, hi - lo), a("wT", lo, hi), A.mult)
-        tt(a("yu", lo, hi), a("xT", lo, hi), a("yt", lo, hi), A.subtract)
-        op("v", lambda e: e.transpose(T.Y[:, lo:hi], T.yu[:, lo:hi]), R=[a("yu", lo, hi)], W=[a("Y", lo, hi)])
+    def sums(j):
+        return a("pb%d" % (c1[j] // 512 % 7), c1[j] % 512, c1[j] % 512 + N1[j])
 
-    pieces = [("s", 0), ("v", 512), ("s", 768), ("s", 1280), ("v", 1792), ("s", 2304), ("s", 2816), ("v", 3328), ("s", 3840),
-              ("s", 4352), ("v", 4864)]
-    slots()
-    message()
-    for k, (q, lo) in enumerate(pieces):
-        hi = (pieces + [("", 8 * CB)])[k + 1][1]
-        gat(q, a("G", lo, hi), VW, a("invP", lo // 16, hi // 16))
-        if k == 1:
-            cp(a("send2"), a("pb7", 0, 48))
-            send(2)
-        for b in range(lo // 128, hi // 128):
-            p0, p1, bank = parts[b // 16]
-            o = 16 * b - p0
-            mm(a(bank, o, o + 16), a("G", 128 * b, 128 * b + 128), a("PosR", 0, 16), True, True)
-        if k == 6:
-            mm(FX, a("NegR"), a("S1"), True, False)
-        if k == 8:
-            arrive(2)
-    finish(0)
-    sca(a("ADD"), a("shU"), a("Rw"))
-    gat("s", a("D1"), a("ADD"), a("SRu"))
-    mm(FX, a("NegR"), a("D1"), False, True)
-    finish(1)
-    finish(2)
-    tt(a("x3s"), a("x2s"), FX, A.add)
-    for k in range(3):
-        sca(a("Y"), a("cpU", 8 * k, 8 * k + 8), a("x3s", 128 * k, 128 * k + 128))
+    def whole(j):
+        n0 = c1[j] // 512 * 512
+        return n0, c1[j + 1], a(sums(j)[0], 0, c1[j + 1] - n0)
+
+    def sum1(j):
+        first = c1[j] % 512 == 0 and "u%d" % (c1[j] // 512) not in opened
+        mm(sums(j), a("NegR"), a("G", c1[j], c1[j + 1]), first, c1[j + 1] % 512 == 0 or j == len(N1) - 1)
+
+    def wslot():
+        gat("s", a("wslot"), a("wrep"), a("LU", 0, 24))
+        compact_copy("wc", "wrep", "dwc")
+        scp(a("KlF"), a("KlB"))
+
+    run(ORDER2, {
+        "v": lambda j: gtt(a("G", c1[j], c1[j + 1]), VW, a("invU", c1[j] // 16, c1[j + 1] // 16), a("wrep", c1[j], c1[j + 1]),
+                           A.mult),
+        "k": sum1,
+        "u": uadd,
+        "e": lambda j: scp(a("win", *whole(j)[:2]), whole(j)[2]),
+        "a": lambda j: tt(a("win", *whole(j)[:2]), whole(j)[2], a("uwin", *whole(j)[:2]), A.add),
+        "slots": lambda: gat("s", a("S1"), VW, a("clU")),
+        "message": lambda: [message(k) for k in range(3)],
+        "send": lambda: send(1, scp),
+        "consts": consts,
+        "dumps": dumps,
+        "out": conn_out,
+        "places": conn_places,
+        "mark": conn_mark,
+        "conn": lambda: ts(a("piU"), a("piT"), 0.25, A.add),
+        "uslot": lambda: gat("s", a("uslot"), a("uwin"), a("LU", 0, 24)),
+        "wslot": wslot,
+        "arrive": lambda: arrive(1),
+        "turn": lambda: scp(a("Rw"), a("pb7", 128, 256), P=64),
+        "add": lambda: sca(a("ADD"), a("shU"), a("Rw")),
+        "total": lambda: gtt(a("D1"), a("ADD"), a("LU", 0, 24), a("S1"), A.subtract),
+        "sum": lambda: mm(a("pb3", 0, 384), a("NegR"), a("D1")),
+        "scale": lambda: tt(a("pb3", 0, 384), a("pb3", 0, 384), a("wslot"), A.mult),
+        "slot": lambda: tt(a("win", M, M + 384), a("uslot"), a("pb3", 0, 384), A.subtract),
+    })
+    compact_copy("x2c", "win", "dx2")
+
+    step = elements(R2, "X2", a("win"), "piU", "KlF", (0, 1, 2, 3))
+    step.update({
+        "order": lambda: gat("s", a("invG"), a("invF"), a("pmU")),
+        "invP": lambda: ts(a("invP"), a("invG"), -1.0, A.mult, E + 0.25, A.add),
+        "compact": compact,
+        "mark": y_mark,
+        "ylist": lambda: ts(a("yU"), a("yF"), 0.25, A.add),
+    })
+    run(ORDER3, step)
+
+    c2 = cuts(N2)
+
+    def slots():
+        for k in range(3):
+            gtt(part("S1", k), VW, a("clU", 8 * k, 8 * k + 8), part("wslot", k), A.mult)
+            message(k)
+
+    def sum2(j):
+        for b in range(c2[j] // 128, c2[j + 1] // 128):
+            k = max(k for k in range(len(FIN) - 1) if FIN[k] <= 16 * b)
+            o = 16 * b - FIN[k]
+            mm(a("pb%d" % k, o, o + 16), a("G", 128 * b, 128 * b + 128), a("NegR", 0, 16))
+
+    def turned(k):
+        return a("pb%d" % k, 256, 256 + FIN[k + 1] - FIN[k])
+
+    def rows(k):
+        s = a("pb%d" % k, 0, FIN[k + 1] - FIN[k])
+        op("v", lambda e: e.transpose(ap(turned(k)), ap(s)), R=[s], W=[turned(k)])
+
+    run(ORDER4, {
+        "s": lambda j: gat("s", a("G", c2[j], c2[j + 1]), VW, a("invP", c2[j] // 16, c2[j + 1] // 16)),
+        "v": lambda j: gat("v", a("G", c2[j], c2[j + 1]), VW, a("invP", c2[j] // 16, c2[j + 1] // 16)),
+        "k": sum2,
+        "t": rows,
+        "w": lambda k: tt(turned(k), turned(k), a("wc", FIN[k], FIN[k + 1]), A.mult),
+        "x": lambda k: tt(a("Y", FIN[k], FIN[k + 1]), turned(k), a("x2c", FIN[k], FIN[k + 1]), A.add),
+        "slots": slots,
+        "send": lambda: send(2, cp),
+        "sends": lambda: send(2, scp),
+        "arrive": lambda: arrive(2),
+        "turn": lambda: cp(a("Rw"), a("pb7", 128, 256), P=64),
+        "turns": lambda: scp(a("Rw"), a("pb7", 128, 256), P=64),
+        "add": lambda: sca(a("ADD"), a("shU"), a("Rw")),
+        "total": total,
+        "sum": lambda k: mm(a("pb%d" % (4 + k), 0, 128), a("NegR"), part("D1", k)),
+        "slot": lambda k: tt(a("Y", CB + 128 * k, CB + 128 * k + 128), a("win", M + 128 * k, M + 128 * k + 128),
+                             a("pb%d" % (4 + k), 0, 128), A.subtract),
+    })
+    gat("v", a("x2c", 0, CB // 2), a("Y"), a("yU", 0, CB // 32))
+    gat("s", a("x2c", CB // 2, CB), a("Y"), a("yU", CB // 32, CB // 16))
     for c in range(8):
-        n = min(CB, M - CB * c)
-        dma("y" if c % 2 == 0 else "s", "dy",
-            lambda e, c=c, n=n: e.dma_start(T.y[:, CB * c:CB * c + n], T.Y[16 * c:16 * c + 16, 0:n]), R=[a("Y", 0, CB)])
+        n0 = place(c)
+        n = min(CB, M - n0)
+        dma("y" if c % 2 == 0 else "s", "dy", T.y[:, n0:n0 + n], T.x2c[16 * c:16 * c + 16, 0:n], R=[a("x2c")])
 
     wait("g", [(name, count[name]) for name in sorted(count)])

@@ -7,48 +7,77 @@ F = ActivationFunctionType
 E, M, CAPP = 4096, 4928, 128
 MW = M + CAPP
 RUN = MW // 16
-ES = 2016
-D0 = 384
+ES = 2240
+D0 = 512
+SC = 1024
 CB = 640
-AF = 3160
+CD = 352
+ND = 8 * CD
+ZC = 632
 PER = 4
-SG = 0
-SD = (SG, 2048, E)
-WD = (0, 1536, 3072, M)
+SD = (0, 2048, E)
+WT = ((0, 1536), (1536, M))
+WP = ((0, 1536), (1536, 3072), (3072, M))
 
-R1 = [512, 512, 256, 256] + [512] * 4 + [256, 256]
-ORDER1 = ("s0 k0 s1 k1 addS lists v2 s3 m0 s4 mask k3 k2 m1 s5 addV m2 m3 invU invF k4 m4 pick k5 m5 u0 u2 mark s6 k6 m6 sum "
-          "s7 u3 k7 s8 k8 keep u1 s9 k9 m7 u5 m8 u6 m9 u4")
-N1 = [256, 256] + [512] * 8 + [320]
-ORDER2 = ("slots v0 k0 message send dumps v1 out k1 consts v2 k2 v3 k3 v4 places k4 e1 e2 mark0 mark1 mark2 v5 k5 e3 v6 u7 k6 "
-          "v7 arrive k7 wslot turn v8 k8 e4 e5 v9 add uslot u8 k9 e6 e7 total v10 sum e8 e9 k10 conn scale slot a10")
-R2 = [128, 128, 256] + [512] * 6 + [256, 256]
-ORDER3 = ("v0 k0 s1 k1 s2 k2 m0 s3 k3 m1 m2 compact s4 k4 m3 mark0 s5 k5 m4 mark1 s6 k6 m5 mark2 s7 k7 m6 s8 k8 order m7 invP "
-          "s9 k9 m8 ylist s10 k10 m9 m10")
-N2 = [512, 256, 512, 512, 512, 512, 512, 512, 512, 512, 256]
-FIN = (0, 224, 416, 544, 640)
-ORDER4 = ("s0 slots v1 send s2 k0 v3 s4 k1 k2 k3 s6 v5 t0 w0 k4 s7 k5 k6 x0 t1 arrive turn w1 add total0 s8 k7 total1 k8 x1 t2 "
-          "total2 s9 s10 k9 k10 w2 sum0 sum1 t3 x2 w3 slot0 slot1 x3 sum2 slot2")
+NA = [512, 512, 256, 256] + [512] * 4 + [256, 256]
+NB = [128, 384, 512, 512, 512, 256, 256, 256]
+FINB = (0, 192, 288, 352)
+BANKB = (4, 5, 6)
+NP = [512, 512, 512, 320, 256]
+BANKP = (0, 1, 2, 3, 5)
+BANKT = (4, 6, 0)
+EARLY = False
+MATCH = False
+NC = [128, 128, 256] + [512] * 6 + [256, 256]
+ND2 = [512, 256, 512, 512, 512, 512, 512, 512, 512, 512, 256]
+FIND = (0, 224, 416, 544, 640)
+OUT = (0, 320, 640)
+STORE = (0, 640)
+ORDER = (
+    "ld sts oneB fz oneF fv fills datA datB key zsy runA0 runA1 runA2 warm zvy shy wy uy0 uy1 stT uy2 uy3 liy stA gAb gas abT negs keT datD datG gBf gIdF gdmp grow zero3 zero4 gIdB gAc zero5 gids grr zero0 zero7 zero1 ybs runB0 kron connU runB1 klb runB2 scatV0 shF scatV1 scatS0 scatS1 tables stB handS handV wT as0 as1 av4 av2 lists ak0 ak2 am0 am2 ak1 as3 ak3 am1 as5 ak5 ak4 uc wP0 out wD wd wP1 am4 am3 am5 addS addV as6 as7 as8 ak7 invF mask dumps as9 uslot am7 ak6 am6 invU u2 u0 ak8 u1 flag ak9 pick am8 invD am9 group keep bv0 bk0 u3 bs7 slots message bv2 bs1 bs3 bk1 bs4 bk2 bk3 bk4 sendv bv5 places pv0 bk5 bt0 bv6 bw0 bk6 mark0 mark1 mark2 back zero2 zero6 bk7 bt1 bx0 bw1 bx1 bt2 bw2 bx2 pk0 pv2 pk2 reps4 wslot order pv4 pv1 arrive turnv pk4 pk1 add total sum consts pv3 conn scale slot pa4 pk3 repy1 repy6 reps2 repy5 repy3 repy7 klf ps0 ps1 ps2 ps3 cs1 cs3 cv0 ck0 ck1 cv2 ck2 ck3 cs4 cs6 cs9 cs10 cs7 cs8 cv5 cm1 cm0 ck5 compact cm2 ymark0 cm5 ck6 ck9 cm3 ymark1 cm6 ck4 cm9 cm4 ymark2 ck7 cm7 invP ck8 cm8 wc yback x2c ck10 cm10 dslot0 ds1 dk1 dslot1 dslot2 ds0 dv2 dk0 dsend ds8 dk2 ds5 ds4 ds6 ds10 ds9 dv3 dk8 dk3 dv7 dt0 dk7 dw0 ylist dt2 dk5 darrive dx0 dw2 dx2 dturnv dadd dk4 dk6 dtotal1 dk10 dsum1 dk9 dtotal2 dt1 dtotal0 dw1 dfin1 dx1 dt3 dsum0 dw3 dfin0 dx3 dsum2 dfin2 yv0 ys1 store0")
+CD = 0
+ND = 8 * CD
+ES = 2016
+NB = []
+FINB = (0,)
+BANKB = ()
+NP = [256, 256] + [512] * 8 + [320]
+BANKP = (0, 1, 2, 3, 4, 5, 6, 0, 1, 2, 3)
+BANKT = (4, 5, 6)
+ORDER = "ld key sts fz zss zvs shy wy uy0 uy1 uy2 uy3 stT wT0 liy stA datA fv warm oneB oneF fills datB gAb gas datG datD grow gIdF gIdB gAc gBf grr gids gdmp zero0 zero1 zero5 zero2 zero7 zero3 zero4 abT neg runA0 runA1 runA2 keT yb kron runB0 shF runB1 connU runB2 klb scatS0 scatS1 scatV0 scatV1 handS handV wT1 stB wP0 wP1 wP2 tables as0 ak0 as1 ak1 addS lists av2 as3 am0 as4 mask ak3 ak2 am1 as5 addV am2 am3 invU invF ak4 am4 pick ak5 am5 u0 u1 flag as6 ak6 out am6 group as7 u3 ak7 as8 ak8 keep u2 as9 ak9 am7 am8 am9 uslot sls0 sls1 sls2 pv0 u5 u6 u4 pv2 msg0 pk0 msg1 msg2 send pk2 pv3 ps0 wslot ps2 dumps klf pk3 pv1 u7 pk1 pv5 pv4 pv8 places ownw2 zero6 consts pk5 pv6 pv10 pv9 pv7 ps1 u9 u8 pk4 pk8 ps5 mark0 pk6 tu1 ps4 tu0 pk9 mark1 mark2 ps3 ps6 ps9 back note ownw0 find1 find0 find2 ownw1 match pk7 tu2 arrive own0 own2 pk10 own1 turn total0 total1 total2 sum0 pa10 conn sum1 finv1 sum2 finv2 ps8 ps7 fins0 cv1 cv0 ck1 ck0 cs2 ck2 cm0 cs3 ck3 cm1 cm2 compact cs4 ck4 cm3 ymark0 cs5 ck5 cm4 ymark1 cs6 ck6 cm5 ymark2 yback x2c wc cs7 ck7 cm6 cs8 ck8 order cm7 invP cs9 ck9 cm8 cs10 ck10 cm9 cm10 dslot0 dslot1 dslot2 ds0 ylist dsendv dv1 ds2 dk0 ds4 dk1 dk2 dv3 dk3 dv5 dk4 ds6 dk5 dk6 dt0 dw0 dv8 dx0 dt1 dw1 dx1 ds7 ds10 dk8 darrive dturnv ds9 dk7 dk10 dk9 dtotal0 dtotal1 dt2 dtotal2 dw2 dsum0 dsum2 dsum1 dx2 dt3 dfin0 dw3 dfin2 dx3 dfin1 yv0 ys1 store0"
+CD = 320
+ND = 8 * CD
+ES = 2112
+NB = [128, 384, 512, 512, 512, 256, 256]
+FINB = (0, 192, 320)
+BANKB = (5, 6)
+NP = [512, 512, 512, 512, 320]
+BANKP = (0, 1, 2, 3, 4)
+BANKT = (5, 6, 0)
+WT = ((0, M),)
+WP = ((2560, 3584), (3584, M), (0, 2560))
+ORDER = "ld fz fv oneB fills shs kes zsy sty datA zvy gas gAb uy0 us1 warm stT keT abT us2 ybs uy3 negs stA runA0 datB runA1 runB0 runA2 scatS0 runB1 shF oneF runB2 datD datG grow gIdB gBf gIdF gdmp gAc zero7 zero1 zero5 grr gids zero3 zero2 zero4 connU kron scatV0 klb scatV1 scatS1 handS handV liy wy as0 stB uc wT0 wP0 wP1 wd wP2 u1 tables ak0 av1 av2 ak1 ak2 addS as5 as3 as4 as6 lists0 am0 ak3 lists1 am1 am2 lists2 am3 addV invF mask ak4 am4 invU invD pick as7 as8 as9 dumps ak5 flag ak6 u2 group am5 am6 ak8 u0 ak9 ak7 keep0 am8 am9 am7 keep1 sls0 sls1 places0 slv2 bv0 out0 u4 msg0 msg1 msg2 bk0 bs4 bs5 bk4 bk5 sendv bs6 bk6 zero0 zero6 bs1 consts bs3 bv2 pv1 places1 out1 bt1 places2 pv0 bk1 bk2 bk3 out2 bw1 places3 bt0 uslot wslot order klf places4 bw0 bx1 bx0 repy3 repy7 repy5 reps2 pk1 pk0 u3 arrive mark0 turn mark1 reps6 mark2 pv3 pk3 pv2 ps0 ps1 ps3 pk2 back repy4 repy1 add whole pv4 pc2 sums pk4 ps4 scale conn slot cv1 cs2 ck1 cs3 cv0 compact0 cm1 compact1 cv5 ck2 ck0 ck3 compact2 ck5 cm2 compact3 cm3 invP cm0 compact4 cm5 ymark0 cs7 cs4 cs9 ck7 ck4 ck9 cm7 cm4 ymark1 cm9 cs6 cs8 cs10 ck6 cm6 ymark2 x2c wc yback ck8 cm8 ck10 cm10 dslot0 dslot1 dslot2 dmsg0 dmsg1 dmsg2 ds0 dv1 dsendv ds2 dk0 dk1 dk2 dv3 dk3 dv5 dt0 ylist dw0 dv8 ds4 dk4 ds6 ds10 ds7 ds9 dk5 dk6 darrive dx0 dt1 dturnv dw1 dadd dk10 dk7 dk8 dk9 dx1 dtotal2 dtotal0 dt2 dtotal1 dt3 dw2 dsum2 dsum1 dsum0 dfin2 dw3 dx2 dfin1 dx3 dfin0 yv0 ys1 store0"
 
 _F = "float32 "
 _B = "bfloat16 "
 _I = "int32 "
 _U = "uint16 "
-_SB = {
-    256: _I + "connI piI " + _U + "connU piU " + _F + "piT " + _B + "oneB",
-    MW: _B + "uwin wrep " + _F + "Wv Ws ADD", M + 384: _F + "win",
-    E: _B + "strep srow X1 " + _F + "X2", 6 * D0: _F + "dat", E + 8: _F + "V", 8 * CB: _F + "G",
-    RUN: _F + "zero invV invS invF", 320: _U + "invU invP " + _F + "invG",
-    128: _F + "oneF NegR IdF KlF Bf Rw frow " + _B + "IdB asB Yb KlB",
-    2: _F + "base", 8: _B + "keB " + _I + "shI " + _U + "shU", 20: _F + "m2 " + _U + "pmU",
-    24: _F + "sh3F dmp dmpS c1 c2 c3 " + _I + "sh3 gid low " + _U + "clU cnU cpU", 72: _I + "LI " + _U + "LU",
-    384: _F + "msk O1 O2 rr ids uslot wslot S1 D1 " + _B + "Ab", 48: _F + "send1 send2", 64: _F + "recv1 recv2",
-    CB: _B + "wc " + _F + "x2c", CB + 240: _F + "Wc", CB + 384: _F + "Y", CB // 16: _F + "yF " + _U + "yU",
-}
+_SB = [
+    (256, _I + "connI piI " + _U + "connU piU " + _F + "piT " + _B + "oneB"),
+    (MW, _B + "uwin wrep " + _F + "Wv Ws ADD"), (M + 384, _F + "win"),
+    (E, _B + "strep X1 " + _F + "X2"), (ES, _F + "dat"), (E + 16, _F + "V"), (8 * CB, _F + "G"),
+    (RUN, _F + "zero invV invS invF"), (320, _U + "invU invP " + _F + "invG"),
+    (128, _F + "oneF NegR IdF KlF Bf frow frowA frowB " + _B + "IdB asB Yb KlB"), (136, _F + "Rw"),
+    (2, _F + "base rot"), (8, _B + "keB"), (20, _F + "m2"), (40, _U + "pmU"),
+    (24, _F + "sh3F dmp dmpS c1 c2 c3 d1 d2 d3 " + _I + "sh3 gid low blk " + _U + "clU cnU cpU mtU"), (80, _I + "LI " + _U + "LU"),
+    (384, _F + "msk O1 O2 rr ids wslot S1 S2 D1 " + _B + "Ab uslot"), (48, _F + "send1 send2"), (64, _F + "recv1 recv2"),
+    (CD + 32, _B + "uc1 wc1"),
+    (CB, _B + "wc " + _F + "x2c yc"), (CB + 240, _F + "Wc"), (CB + 384, _F + "Y"), (CB // 16, _F + "yF " + _U + "yU"),
+]
 SCRATCH = {}
-for _n in _SB:
+for _n, _names in _SB:
     _t = ""
-    for _w in _SB[_n].split():
+    for _w in _names.split():
         if _w + " " in (_F, _B, _I, _U):
             _t = _w
         else:
@@ -56,8 +85,8 @@ for _n in _SB:
 for _k in range(8):
     SCRATCH["pb%d" % _k] = ("psum", [128, 512], "float32")
 
-SEMAPHORES = ["cv", "cs", "ct", "cg", "dconn", "dshare", "dke", "du", "dWs", "dWv", "dsh", "drow", "ds1", "ds2", "ds3", "ds4",
-              "dw1", "dw2", "dw3", "dw4", "dw5", "dw6", "dxv", "dxs", "dwc", "dx2", "dc1", "dc2", "dc3",
+SEMAPHORES = ["cv", "cs", "ct", "cg", "dconn", "dshare", "dke", "du", "dWs", "dWv", "dsh", "ds1", "ds2", "ds3", "ds4",
+              "dw1", "dw2", "dw3", "dw4", "dw5", "dw6", "dxv", "dxs", "dwc", "dx2", "dc1", "dc2", "dc3", "duc", "dwd", "drep",
               "dy", "arr1", "arr2", "loc1", "loc2"]
 
 
@@ -128,6 +157,9 @@ def rank_program(g, core, T, topo):
     def ap(x, P=128):
         return T[x[0]][0:P, x[1]:x[2]]
 
+    def pb(k, lo, hi):
+        return ("pb%d" % k, lo, hi)
+
     def fill(x, val):
         op("v", lambda e: e.memset(ap(x), val), W=[x])
 
@@ -140,14 +172,21 @@ def rank_program(g, core, T, topo):
     def tt(out, in0, in1, o, P=128):
         op("v", lambda e: e.tensor_tensor(ap(out, P), ap(in0, P), ap(in1, P), o), R=[in0, in1], W=[out])
 
-    def cp(out, in_, P=128):
-        op("v", lambda e: e.tensor_copy(ap(out, P), ap(in_, P)), R=[in_], W=[out])
+    def copy(q, out, in_, scale=1.0, P=128):
+        if q == "v" and scale != 1.0:
+            ts(out, in_, scale, A.mult, P=P)
+        elif q == "v":
+            op("v", lambda e: e.tensor_copy(ap(out, P), ap(in_, P)), R=[in_], W=[out])
+        else:
+            op("s", lambda e: e.activation(ap(out, P), ap(in_, P), F.Copy, scale=scale), R=[in_], W=[out])
 
-    def scp(out, in_, scale=1.0, P=128):
-        op("s", lambda e: e.activation(ap(out, P), ap(in_, P), F.Copy, scale=scale), R=[in_], W=[out])
+    def silu(out, in_, bias=0.0):
+        op("s", lambda e: e.activation(ap(out), ap(in_), F.Silu, bias=bias), R=[in_], W=[out])
 
     def gat(q, out, win, off, scale=1.0):
-        if q == "v":
+        if q == "v" and scale != 1.0:
+            op("v", lambda e: e.tensor_scalar(ap(out), ap(win).indirect(ap(off)), scale, None, A.mult), R=[win, off], W=[out])
+        elif q == "v":
             op("v", lambda e: e.tensor_copy(ap(out), ap(win).indirect(ap(off))), R=[win, off], W=[out])
         else:
             op("s", lambda e: e.activation(ap(out), ap(win).indirect(ap(off)), F.Copy, scale=scale), R=[win, off], W=[out])
@@ -155,11 +194,17 @@ def rank_program(g, core, T, topo):
     def gtt(out, win, off, in1, o):
         op("v", lambda e: e.tensor_tensor(ap(out), ap(win).indirect(ap(off)), ap(in1), o), R=[win, off, in1], W=[out])
 
-    def sca(win, off, in_):
-        op("v", lambda e: e.tensor_copy(ap(win).indirect(ap(off)), ap(in_)), R=[off, in_], W=[win])
+    def columns(out, win, off):
+        op("v", lambda e: e.tensor_scalar(ap(out), ap(win).indirect(ap(off)), -1.0, E + 0.25, A.mult, A.add), R=[win, off], W=[out])
 
-    def silu_sca(win, off, in_):
-        op("s", lambda e: e.activation(ap(win).indirect(ap(off)), ap(in_), F.Silu), R=[off, in_], W=[win])
+    def sca(q, win, off, in_, add=None, times=1.0):
+        if q == "s":
+            op("s", lambda e: e.activation(ap(win).indirect(ap(off)), ap(in_), F.Silu), R=[off, in_], W=[win])
+        elif add is None:
+            op("v", lambda e: e.tensor_copy(ap(win).indirect(ap(off)), ap(in_)), R=[off, in_], W=[win])
+        else:
+            op("v", lambda e: e.tensor_scalar(ap(win).indirect(ap(off)), ap(in_), times, float(add), A.mult, A.add),
+               R=[off, in_], W=[win])
 
     def mm(out, lhsT, rhs, start=True, stop=True, K=128, P=128, extra=()):
         op("t", lambda e: e.matmul(ap(out, P), ap(lhsT, K), ap(rhs, K), start, stop), R=[lhsT, rhs], W=[out], acc=not start,
@@ -179,16 +224,11 @@ def rank_program(g, core, T, topo):
         gop(lambda e: e.affine_select(T[out[0]][p0:p0 + P, out[1]:out[2]], T[in_[0]][p0:p0 + P, in_[1]:in_[2]], pattern, cmp,
                                       other, base, cm), [in_], [out], p0 > 0)
 
-    def run(order, step):
-        for w in order.split():
-            name = w.rstrip("0123456789")
-            if name == w:
-                step[w]()
-            else:
-                step[name](int(w[len(name):]))
+    def staged(calls):
+        return lambda k: next(calls)
 
-    def cuts(widths):
-        c = [0]
+    def cuts(widths, first=0):
+        c = [first]
         for n in widths:
             c.append(c[-1] + n)
         return c
@@ -201,152 +241,193 @@ def rank_program(g, core, T, topo):
         else:
             d, n = ((32, 8), (4, 4))[step - 1]
             for m in range(1, n):
-                dma(q, sem, T[nm][m * d // n:128:d, lo:hi], T[nm][0:128:d, lo:hi], R=[x], W=[x])
+                dma(q, sem, T[nm][m * d // n:128:d, lo:hi], T[nm][0:128:d, lo:hi], R=[x], W=[x] + [(nm + "4", lo, hi)] * (step == 1))
 
-    dma("y", "dconn", T.connI[:], T.conn[:], W=[a("connI")])
-    dma("y", "dke", T.keB[0:8, :], T.ke[:], W=[a("keB")])
-    if SG:
-        dma("s", "drow", T.srow[0:1, 0:SG], T.st[0:1, 0:SG], W=[a("srow")])
-    spread("s", "ds1", 0, "strep", "st", SG, E)
-    fill(a("zero"), 0.0)
-    for wn in ("Ws", "Wv"):
-        dma("s", "d" + wn, T[wn][0:128:16, :], T.zero[:], R=[a("zero")], W=[a(wn)])
-    for k, q in enumerate(partners):
-        dma("y", "dshare", T.sh3[0:16, 8 * k:8 * k + 8], T.share[16 * q:16 * q + 16, :], W=[a("sh3")])
-    spread("y", "dw1", 0, "wrep", "w", 0, M)
-    for c in range(8):
-        dma("y", "du", T.uwin[16 * c:16 * c + 16, 0:M], T.u[:], W=[a("uwin", 0, M)])
-    spread("y", "ds2", 1, "strep", "st", SG, E)
-    spread("y", "dw2", 1, "wrep", "w", WD[0], WD[1])
-    dma("y", "dsh", T.shI[:], T.share[:], W=[a("shI")])
-    spread("y", "ds3", 2, "strep", "st", SD[0], SD[1])
+    NEG = a("NegR")
+    VW = a("V")
+    SH = a("LU", 72, 80)
+    cp = cuts(NP, ND)
+    step = {}
 
-    iota(a("dat", 0, D0), [[-1, D0]], E, 0)
-    fill(a("oneB"), 1.0)
-    fill(a("oneF"), 1.0)
-    select(a("Ab", 0, 128), a("oneB", 0, 128), [[0, 8], [-1, 16]], A.is_equal, 0, 1, P=16)
-    select(a("asB"), a("oneB", 0, 128), [[-1, 8], [0, 16]], A.is_equal, 0, 1, P=8)
-    iota(a("frow"), [[0, 8], [40, 8], [1, 2]], 0, 0, 0, 1)
-    iota(a("m2"), [[2, 20]], 0, 0, 0, 1)
-    for x0 in range(0, SG, 512):
-        gop(lambda e: e.partition_broadcast(T.strep[:, x0:x0 + 512], T.srow[0:1, x0:x0 + 512], 128), [a("srow")],
-            [a("strep", x0, x0 + 512)], True)
-    select(a("IdF"), a("oneF"), [[-1, 128]], A.is_equal, 0, 1)
-    select(a("IdB"), a("oneB", 0, 128), [[-1, 128]], A.is_equal, 0, 1)
-    select(a("Ab", 128, 384), a("oneB"), [[0, 16], [-1, 16]], A.is_equal, 0, 1, P=16)
-    select(a("Bf"), a("oneF"), [[-16, 8], [0, 16]], A.is_ge, 0, 1)
-    select(a("Bf"), a("Bf"), [[16, 8], [0, 16]], A.is_ge, 15, -1)
-    iota(a("rr"), [[0, 24], [32767, 16]], 0, 0)
-    for z in (a("V", E, E + 8), a("recv1", 16 * r, 16 * r + 16), a("recv2", 16 * r, 16 * r + 16), a("uwin", M, MW),
-              a("wrep", M, MW)):
-        iota(z, [[0, z[2] - z[1]]], 0, 0)
-    iota(a("ids"), [[1, 384]], M, 0)
-    iota(a("dmpS"), [[0, 3], [16, 8]], E, 1)
-    iota(a("Rw"), [[0, 128]], 0, 0, 64, 128)
+    def shares(q):
+        for k, p in enumerate(partners):
+            dma(q, "dshare", T.sh3[0:16, 8 * k:8 * k + 8], T.share[16 * p:16 * p + 16, :], W=[a("sh3")])
 
-    def fill_add(lo, hi):
-        for x0 in range(lo, hi, 632):
-            iota(a("ADD", x0, x0 + 632), [[0, 632]], 0, 0)
+    def load_u(q, k):
+        for c in range(2 * k, 2 * k + 2):
+            dma(q, "du", T.uwin[16 * c:16 * c + 16, 0:M], T.u[:], W=[a("uwin", 0, M)])
 
-    fill_add(0, AF)
-    ts(a("dat", D0, 2 * D0), a("dat", 0, D0), float(-D0), A.add)
-    ts(a("dat", 2 * D0, 4 * D0), a("dat", 0, 2 * D0), float(-2 * D0), A.add)
-    for k in (4, 5):
-        x, y = a("dat", k * D0, k * D0 + D0), a("dat", 0, D0)
-        op("s", lambda e, x=x, y=y, k=k: e.activation(ap(x), ap(y), F.Silu, bias=float(-k * D0)), R=[y], W=[x])
-    mm(a("pb0", 0, 128), a("Ab", 0, 128), a("Ab", 0, 128), K=16)
-    ts(a("NegR"), a("pb0", 0, 128), -1.0, A.mult)
+    for q in "ys":
+        step.update({
+            "ke" + q: lambda q=q: dma(q, "dke", T.keB[0:8, :], T.ke[:], W=[a("keB")]),
+            "sh" + q: lambda q=q: shares(q),
+            "li" + q: lambda q=q: dma(q, "dsh", T.LI[:, 72:80], T.share[:], W=[a("LI", 72, 80)]),
+            "zs" + q: lambda q=q: dma(q, "dWs", T.Ws[0:128:16, :], T.zero[:], R=[a("zero")], W=[a("Ws")]),
+            "zv" + q: lambda q=q: dma(q, "dWv", T.Wv[0:128:16, :], T.zero[:], R=[a("zero")], W=[a("Wv")]),
+            "st" + q: lambda q=q: spread(q, "ds1", 0, "strep", "st", 0, E),
+            "w" + q: lambda q=q: spread(q, "dw1", 0, "wrep", "w", 0, M),
+            "u" + q: lambda k, q=q: load_u(q, k),
+        })
+
+    def numbers(lo, hi):
+        iota(a("dat", lo, hi), [[-1, hi - lo]], E - lo, 0)
+
+    def fills():
+        for z in (a("recv2", 16 * r, 16 * r + 16), a("uwin", M, MW), a("wrep", M, MW)):
+            fill(z, 0.0)
+        fill(a("Rw"), 0.0)
+
+    def rows():
+        iota(a("frow"), [[0, 8], [40, 8], [1, 2]], 0, 0, 0, 1)
+        iota(a("m2"), [[2, 20]], 0, 0, 0, 1)
+        if CD:
+            iota(a("frowA"), [[0, 8], [CD // 16, 2], [0, 8]], 0, 0, 0, 1)
+            iota(a("frowB"), [[0, 16], [CD // 8, 4], [1, 2]], 0, 0, 0, 1)
+
+    def blocks():
+        select(a("Bf"), a("oneF"), [[-16, 8], [0, 16]], A.is_ge, 0, 1)
+        select(a("Bf"), a("Bf"), [[16, 8], [0, 16]], A.is_ge, 15, -1)
+
+    step.update({
+        "ld": lambda: dma("y", "dconn", T.connI[:], T.conn[:], W=[a("connI")]),
+        "stT": lambda: spread("y", "ds2", 1, "strep", "st", 0, E),
+        "wT": lambda k: spread("y", "dw%d" % (2 + k), 1, "wrep", "w", *WT[k]),
+        "fv": lambda: fill(a("V", E, E + 16), 0.0),
+        "warm": lambda: silu(a("recv1", 16 * r, 16 * r + 16), a("V", E, E + 16)),
+        "fz": lambda: fill(a("zero"), 0.0),
+        "oneB": lambda: fill(a("oneB"), 1.0),
+        "oneF": lambda: fill(a("oneF"), 1.0),
+        "fills": fills,
+        "datA": lambda: numbers(0, D0),
+        "datB": lambda: ts(a("dat", D0, 2 * D0), a("dat", 0, D0), float(-D0), A.add),
+        "datC": lambda: silu(a("dat", 2 * D0, 3 * D0), a("dat", 0, D0), float(-2 * D0)),
+        "datG": lambda: numbers(2 * D0, 3 * D0),
+        "datD": lambda: numbers(3 * D0, ES),
+        "gAb": lambda: select(a("Ab", 0, 128), a("oneB", 0, 128), [[0, 8], [-1, 16]], A.is_equal, 0, 1, P=16),
+        "gas": lambda: select(a("asB"), a("oneB", 0, 128), [[-1, 8], [0, 16]], A.is_equal, 0, 1, P=8),
+        "grow": rows,
+        "gIdF": lambda: select(a("IdF"), a("oneF"), [[-1, 128]], A.is_equal, 0, 1),
+        "gIdB": lambda: select(a("IdB"), a("oneB", 0, 128), [[-1, 128]], A.is_equal, 0, 1),
+        "gAc": lambda: select(a("Ab", 128, 384), a("oneB"), [[0, 16], [-1, 16]], A.is_equal, 0, 1, P=16),
+        "gBf": blocks,
+        "grr": lambda: iota(a("rr"), [[0, 24], [32767, 16]], 0, 0),
+        "gids": lambda: iota(a("ids"), [[1, 384]], M, 0),
+        "gdmp": lambda: iota(a("dmpS"), [[0, 3], [16, 8]], E, 1),
+        "abT": lambda: mm(pb(0, 0, 128), a("Ab", 0, 128), a("Ab", 0, 128), K=16),
+    })
 
     def runs(k, lo, hi):
         if k == 0:
             ts(a("piI", lo, hi), a("connI", lo, hi), 15, A.bitwise_and)
-            ts(a("pb6", lo, hi), a("connI", lo, hi), 1.0 / (16 * RUN - 1), A.mult)
+            ts(pb(6, lo, hi), a("connI", lo, hi), 1.0 / (16 * RUN - 1), A.mult)
         elif k == 1:
-            tt(a("piT", lo, hi), a("pb6", lo, hi), a("piI", lo, hi), A.add)
+            tt(a("piT", lo, hi), pb(6, lo, hi), a("piI", lo, hi), A.add)
         else:
             ts(a("piU", lo, hi), a("piT", lo, hi), (16 * RUN - 1) / 16.0, A.mult, 0.25, A.add)
 
-    for k in range(3):
-        runs(k, 0, ES // 16)
-    mm(a("pb1", 0, 128), a("keB"), a("asB"), K=8, P=8)
-    ts(a("Yb"), a("pb1", 0, 128), -1.0, A.mult, P=8)
-    mm(a("pb2", 0, 128), a("asB"), a("Yb"), K=8)
-    runs(0, ES // 16, E // 16)
-    cp(a("sh3F"), a("sh3"), P=16)
-    runs(1, ES // 16, E // 16)
-    cp(a("connU"), a("connI"))
-    runs(2, ES // 16, E // 16)
-    tt(a("KlB"), a("pb2", 0, 128), a("NegR"), A.mult)
+    cs, cv = (0, SC, ES), (ES, ES + (E - ES) // 64 * 32, E)
 
-    silu_sca(a("Ws"), a("piU", 0, ES // 16), a("dat", 0, ES))
-    off, x = a("piU", ES // 16, E // 16), a("dat", 0, E - ES)
-    op("v", lambda e: e.tensor_scalar(ap(a("Wv")).indirect(ap(off)), ap(x), 1.0, float(-ES), A.mult, A.add),
-       R=[off, x], W=[a("Wv")])
-    dma("y", "dxs", T.invS[:], T.Ws[0:128:16, :], R=[a("Ws")], W=[a("invS")])
-    dma("y", "dxv", T.invV[:], T.Wv[0:128:16, :], R=[a("Wv")], W=[a("invV")])
-    spread("y", "dw3", 1, "wrep", "w", WD[1], M)
-    spread("y", "ds4", 2, "strep", "st", SD[1], SD[2])
-    for k in range(len(WD) - 1):
-        spread("y", "dw%d" % (4 + k), 2, "wrep", "w", WD[k], WD[k + 1])
+    def compact_u():
+        for c in range(8):
+            dma("y", "duc", T.uc1[16 * c:16 * c + 16, 0:CD], T.u[:, CD * c:CD * c + CD], W=[a("uc1")])
 
-    mm(a("pb3", 0, 24), a("NegR"), a("sh3F"), K=16)
-    mm(a("pb3", 32, 52), a("frow"), a("oneF", 0, 20), True, False, K=1)
-    mm(a("pb3", 32, 52), a("oneF"), a("m2"), False, True, K=1)
-    SR = [a("LU", 8 * k, 8 * k + 8) for k in range(3)]
+    def compact_w():
+        for c in range(8):
+            dma("y", "dwd", T.wc1[16 * c:16 * c + 16, 0:CD], T.wrep[0:64:4, CD * c:CD * c + CD], R=[("wrep4", 0, ND)], W=[a("wc1")])
+
+    def tables():
+        mm(pb(3, 0, 24), NEG, a("sh3F"), K=16)
+        mm(pb(3, 32, 52), a("frow"), a("oneF", 0, 20), True, False, K=1)
+        mm(pb(3, 32, 52), a("oneF"), a("m2"), False, True, K=1)
+        if CD:
+            x = pb(3, 52, 52 + CD // 32)
+            mm(x, a("frowA"), a("oneF", 0, CD // 32), True, False, K=1)
+            mm(x, a("frowB"), a("oneF", 0, CD // 32), False, False, K=1)
+            mm(x, a("oneF"), a("m2", 0, CD // 32), False, True, K=1)
+            mm(pb(3, 24, 26), a("Bf"), a("dmpS", 0, 2))
 
     def lists():
-        ts(a("LI", 0, 24), a("pb3", 0, 24), -1.0, A.mult)
-        ts(a("pmU"), a("pb3", 32, 52), float(M // 16), A.min, 0.25, A.add)
+        if CD:
+            ts(a("rot"), pb(3, 24, 26), -16.0 * E - 120, A.add, CD / 256.0, A.mult)
+        ts(a("LI", 0, 24), pb(3, 0, 24), -1.0, A.mult)
+        ts(a("pmU", 0, 20 + CD // 32), pb(3, 32, 52 + CD // 32), float(M // 16), A.min, 0.25, A.add)
+        yield
         ts(a("LI", 24, 48), a("LI", 0, 24), 4, A.arith_shift_right)
         ts(a("LI", 48, 72), a("LI", 0, 24), 15, A.bitwise_and)
-        cp(a("shU"), a("shI"))
-        cp(a("LU"), a("LI"))
+        yield
+        copy("v", a("LU"), a("LI"))
+        yield
 
-    def dumps():
-        scp(a("dmpS"), a("dmpS"), 16.0 / (E - 1))
+    step.update({
+        "runA": lambda k: runs(k, 0, ES // 16),
+        "runB": lambda k: runs(k, ES // 16, E // 16),
+        "neg": lambda: ts(NEG, pb(0, 0, 128), -1.0, A.mult),
+        "negs": lambda: copy("s", NEG, pb(0, 0, 128), -1.0),
+        "keT": lambda: mm(pb(1, 0, 128), a("keB"), a("asB"), K=8, P=8),
+        "yb": lambda: ts(a("Yb"), pb(1, 0, 128), -1.0, A.mult, P=8),
+        "ybs": lambda: copy("s", a("Yb"), pb(1, 0, 128), -1.0, P=8),
+        "kron": lambda: mm(pb(2, 0, 128), a("asB"), a("Yb"), K=8),
+        "klb": lambda: tt(a("KlB"), pb(2, 0, 128), NEG, A.mult),
+        "shF": lambda: copy("v", a("sh3F"), a("sh3"), P=16),
+        "connU": lambda: copy("v", a("connU"), a("connI")),
+        "scatS": lambda k: sca("s", a("Ws"), a("piU", cs[k] // 16, cs[k + 1] // 16), a("dat", cs[k], cs[k + 1])),
+        "scatV": lambda k: sca("v", a("Wv"), a("piU", cv[k] // 16, cv[k + 1] // 16), a("dat", 0, cv[k + 1] - cv[k]), -cv[k]),
+        "handS": lambda: dma("y", "dxs", T.invS[:], T.Ws[0:128:16, :], R=[a("Ws")], W=[a("invS")]),
+        "handV": lambda: dma("y", "dxv", T.invV[:], T.Wv[0:128:16, :], R=[a("Wv")], W=[a("invV")]),
+        "stA": lambda: spread("y", "ds3", 2, "strep", "st", SD[0], SD[1]),
+        "stB": lambda: spread("y", "ds4", 2, "strep", "st", SD[1], SD[2]),
+        "uc": compact_u,
+        "wd": compact_w,
+        "wP": lambda k: spread("y", "dw%d" % (4 + k), 2, "wrep", "w", *WP[k]),
+        "zero": lambda k: iota(a("ADD", ZC * k, ZC * k + ZC), [[0, ZC]], 0, 0),
+        "tables": tables,
+        "lists": staged(lists()),
+    })
 
-    IV = a("pb7", 0, RUN)
-    CL = a("pb7", 0, 384)
+    IV = pb(7, 0, RUN)
+    CL = pb(7, 0, 384)
 
-    def uadd(c):
-        n0, n1 = 512 * c, min(512 * c + 512, M)
-        mm(a("pb%d" % (c % 7), 0, n1 - n0), a("IdB"), a("uwin", n0, n1), True, False)
+    def sums(j):
+        return pb(BANKP[j], 0, NP[j])
 
-    def keep():
-        op("v", lambda e: e.tensor_tensor_scan(ap(a("O2")), ap(a("rr")), ap(CL), 0.0, A.min, A.max),
-           R=[a("rr"), CL], W=[a("O2")])
-        op("v", lambda e: e.tensor_scalar(ap(a("clU")), T.O2[:, 15:384:16], -16384.0, 16384 + E + 0.25, A.mult, A.add),
-           R=[a("O2")], W=[a("clU")])
+    def diagonal(rows, tmp, out, s1, s2):
+        op("v", lambda e: e.tensor_tensor_scan(ap(tmp), ap(a("rr")), ap(rows), 0.0, A.min, A.max), R=[a("rr"), rows], W=[tmp])
+        yield
+        op("v", lambda e: e.tensor_scalar(ap(out), T[tmp[0]][:, 15:384:16], s1, s2, A.mult, A.add), R=[tmp], W=[out])
+        yield
 
-    def elements(widths, X, win, lst, K, banks):
+    def gathers(ph, widths, out, win, lst):
         c = cuts(widths)
+        for q in "sv":
+            step[ph + q] = lambda j, q=q: gat(q, a(out, c[j], c[j + 1]), win, a(lst, c[j] // 16, c[j + 1] // 16))
+        return c
+
+    def elements(ph, widths, X, win, lst, K, banks):
+        c = gathers(ph, widths, X, win, lst)
 
         def bank(j):
-            return a("pb%d" % banks[j % len(banks)], 0, widths[j])
-        return {
-            "s": lambda j: gat("s", a(X, c[j], c[j + 1]), win, a(lst, c[j] // 16, c[j + 1] // 16)),
-            "v": lambda j: gat("v", a(X, c[j], c[j + 1]), win, a(lst, c[j] // 16, c[j + 1] // 16)),
-            "k": lambda j: mm(bank(j), a(K), a(X, c[j], c[j + 1])),
-            "m": lambda j: tt(a("V", c[j], c[j + 1]), bank(j), a("strep", c[j], c[j + 1]), A.mult),
-        }
+            return pb(banks[j % len(banks)], 0, widths[j])
+        step[ph + "k"] = lambda j: mm(bank(j), a(K), a(X, c[j], c[j + 1]))
+        step[ph + "m"] = lambda j: tt(a("V", c[j], c[j + 1]), bank(j), a("strep", c[j], c[j + 1]), A.mult)
 
-    step = elements(R1, "X1", a("uwin", 0, M), "connU", "KlB", (4, 5, 6))
+    elements("a", NA, "X1", a("uwin", 0, M), "connU", "KlB", (4, 5, 6))
+    elements("c", NC, "X2", a("win"), "piU", "KlF", (0, 1, 2, 3))
     step.update({
-        "u": uadd,
-        "lists": lists,
+        "u": lambda j: mm(sums(j), a("IdB"), a("uwin", cp[j], cp[j + 1]), True, False),
         "mask": lambda: gat("s", a("msk"), a("NegR", 0, 16), a("LU", 48, 72), -1.0 / 16384),
+        "maskv": lambda: gat("v", a("msk"), a("NegR", 0, 16), a("LU", 48, 72), -1.0 / 16384),
         "addS": lambda: mm(IV, a("IdF"), a("invS"), True, False),
         "addV": lambda: mm(IV, a("IdF"), a("invV"), False, True),
-        "invU": lambda: ts(a("invU", 0, RUN), IV, -1.0, A.mult, E + 0.25, A.add),
-        "invF": lambda: scp(a("invF"), IV),
+        "invU": lambda: ts(a("invU", ND // 16, M // 16), pb(7, ND // 16, M // 16), -1.0, A.mult, E + 0.25, A.add),
+        "invD": lambda: columns(a("invU", 0, ND // 16), a("invF"), a("pmU", 20, 20 + CD // 32)),
+        "invF": lambda: copy("s", a("invF"), IV),
+        "invFv": lambda: copy("v", a("invF"), IV),
         "pick": lambda: gtt(a("O1"), a("invF"), a("LU", 24, 48), a("msk"), A.mult),
-        "mark": lambda: mm(CL, a("Ab", 0, 128), a("Ab"), True, False, K=16),
-        "sum": lambda: mm(CL, a("Bf"), a("O1"), False, True),
-        "keep": keep,
+        "flag": lambda: mm(CL, a("Ab", 0, 128), a("Ab"), True, False, K=16),
+        "group": lambda: mm(CL, a("Bf"), a("O1"), False, True),
+        "keep": staged(diagonal(CL, a("O2"), a("clU"), -16384.0, 16384 + E + 0.25)),
     })
-    run(ORDER1, step)
 
-    VW = a("V")
     used, masks = [], {}
     for q in sorted(partners, key=lambda q: len(topo.engines(core, T.cores[q]))):
         ok = [e for e in topo.engines(core, T.cores[q]) if e not in used][:PER]
@@ -356,12 +437,15 @@ def rank_program(g, core, T, topo):
     def part(nm, k):
         return a(nm, 128 * k, 128 * k + 128)
 
-    def message(k):
-        mm(a("pb7", 16 * k, 16 * k + 16), part("S1", k), a("NegR", 0, 16))
+    def third(nm, k):
+        return a(nm, 8 * k, 8 * k + 8)
 
-    def send(rnd, copy):
+    def message(k):
+        mm(pb(7, 16 * k, 16 * k + 16), part("S1", k), a("NegR", 0, 16))
+
+    def send(rnd, by):
         nm = "send%d" % rnd
-        copy(a(nm), a("pb7", 0, 48))
+        copy(by, a(nm), pb(7, 0, 48))
         wait("g", needs("g", [a(nm)], [], "loc%d" % rnd, False))
         tr = []
         for k, q in enumerate(partners):
@@ -374,10 +458,7 @@ def rank_program(g, core, T, topo):
         count["arr%d" % rnd] = 3 * PER
 
     def arrive(rnd):
-        mm(a("pb7", 128, 256), a("recv%d" % rnd), a("IdF"), P=64, extra=[("arr%d" % rnd, 3 * PER)])
-
-    def total(k):
-        gtt(part("D1", k), a("ADD"), SR[k], part("S1", k), A.subtract)
+        mm(pb(7, 128, 256), a("recv%d" % rnd), a("IdF"), P=64, extra=[("arr%d" % rnd, 3 * PER)])
 
     def place(c):
         return CB * (4 * (c % 2) + c // 2)
@@ -386,12 +467,11 @@ def rank_program(g, core, T, topo):
         for c in range(8):
             n0 = place(c)
             n = min(CB, M - n0)
-            dma("y", sem, T[nm][16 * c:16 * c + 16, 0:n], T[src][16 * c:16 * c + 16, n0:n0 + n], R=[a(src, 0, M)], W=[a(nm)])
+            dma("y", sem, T[nm][16 * c:16 * c + 16, 0:n], T[src][0:16, n0:n0 + n], R=[a(src, 0, M)], W=[a(nm)])
 
     def consts():
-        fill_add(AF, MW)
         iota(a("dmp"), [[0, 3], [16, 8]], CB, 1)
-        iota(a("Wc", 0, CB), [[1, 16], [16, CB // 16]], 0, 0)
+        iota(a("Wc", 0, CB), [[1, 16], [16, CB // 16]], 384, 0)
         for k in range(4):
             iota(a("base"), [[0, 2]], place(2 * k + 1) // 16, 0, 32 * k, 32 * k + 32)
             select(a("base"), a("base"), [[0, 2]], A.is_ge, -16, 1, 32, 32 * k, float(place(2 * k) // 16))
@@ -399,8 +479,18 @@ def rank_program(g, core, T, topo):
             iota(a(nm, 448, CB), [[0, CB - 448]], 0, 0, 96, 128)
 
     def conn_out():
-        cp(a("piT"), a("connI"))
+        x, y, rot = pb(3, 0, 256), pb(3, 256, 512), T.rot[:, 0:1]
+        if CD:
+            ts(x, a("connI"), float(ND), A.is_lt, rot, A.mult, R=[a("rot")])
+            ts(y, a("connI"), rot, A.is_lt, float(ND), A.mult, R=[a("rot")])
+            yield
+            tt(a("piT"), a("connI"), x, A.subtract)
+            yield
+            tt(a("piT"), a("piT"), y, A.add)
+        else:
+            copy("v", a("piT"), a("connI"))
         dma("y", "dc1", T.Ws[0:128:16, 0:E], T.piT[:], R=[a("piT")], W=[a("Ws")])
+        yield
 
     def conn_places():
         last = T.O2[:, 15:384:16]
@@ -410,136 +500,162 @@ def rank_program(g, core, T, topo):
         from_last(a("gid"), -16384.0, 16384.0 + E)
         from_last(a("c1"), -16384.0 / (E - 1), (16384.0 + E) / (E - 1))
         from_last(a("c2"), -2.0 ** 20, 2.0 ** 20 + 64)
+        yield
         ts(a("low"), a("gid"), 15, A.bitwise_and)
         tt(a("c2"), a("c2"), a("dmpS"), A.min)
+        yield
         tt(a("c1"), a("c1"), a("low"), A.add)
+        yield
         tt(a("c3"), a("c1"), a("c2"), A.max)
+        yield
         ts(a("cnU"), a("c3"), (E - 1) / 16.0, A.mult, 0.25, A.add)
-
-    def conn_mark(k):
-        silu_sca(a("Ws"), a("cnU", 8 * k, 8 * k + 8), part("ids", k))
-        if k == 2:
-            dma("y", "dc2", T.piT[:], T.Ws[0:128:16, 0:E], R=[a("Ws")], W=[a("piT")])
+        yield
 
     def compact():
         b = T.base[:, 0:1]
-        ts(a("gid"), a("LI", 0, 24), 1.0 / CB, A.mult, -0.4992, A.add)
-        ts(a("c1"), a("LI", 48, 72), float(CB // 16), A.mult, b, A.subtract, R=[a("base")])
-        tt(a("c3"), a("LI", 24, 48), a("dmp"), A.subtract)
-        ts(a("c2"), a("gid"), float(CB // 16), A.mult, b, A.is_equal, R=[a("base")])
-        tt(a("c1"), a("c1"), a("c3"), A.add)
-        tt(a("c1"), a("c1"), a("c2"), A.mult)
-        tt(a("c1"), a("c1"), a("dmp"), A.add)
-        cp(a("cpU"), a("c1"))
+        ts(a("blk"), a("LI", 0, 24), 1.0 / CB, A.mult, -0.4992, A.add)
+        ts(a("d1"), a("LI", 48, 72), float(CB // 16), A.mult, b, A.subtract, R=[a("base")])
+        tt(a("d3"), a("LI", 24, 48), a("dmp"), A.subtract)
+        yield
+        ts(a("d2"), a("blk"), float(CB // 16), A.mult, b, A.is_equal, R=[a("base")])
+        tt(a("d1"), a("d1"), a("d3"), A.add)
+        yield
+        tt(a("d1"), a("d1"), a("d2"), A.mult)
+        yield
+        tt(a("d1"), a("d1"), a("dmp"), A.add)
+        yield
+        copy("v", a("cpU"), a("d1"))
+        yield
 
-    def y_mark(k):
-        off, x = a("cpU", 8 * k, 8 * k + 8), part("ids", k)
-        op("v", lambda e: e.tensor_scalar(ap(a("Wc")).indirect(ap(off)), ap(x), 1.0, float(CB - M), A.mult, A.add),
-           R=[off, x], W=[a("Wc")])
-        if k == 2:
-            dma("y", "dc3", T.yF[:], T.Wc[0:128:16, 0:CB], R=[a("Wc")], W=[a("yF")])
+    def finish(ph, fin, banks, w, old, out, first):
+        def turned(k):
+            return pb(banks[k], 256, 256 + fin[k + 1] - fin[k])
 
-    c1 = cuts(N1)
-    opened = set(w for w in (ORDER1 + " " + ORDER2).split() if w[0] == "u")
+        def rows(k):
+            s = pb(banks[k], 0, fin[k + 1] - fin[k])
+            op("v", lambda e: e.transpose(ap(turned(k)), ap(s)), R=[s], W=[turned(k)])
+        step[ph + "t"] = rows
+        step[ph + "w"] = lambda k: tt(turned(k), turned(k), a(w, fin[k], fin[k + 1]), A.mult)
+        step[ph + "x"] = lambda k: tt(a(out, first + fin[k], first + fin[k + 1]), turned(k), a(old, fin[k], fin[k + 1]), A.add)
 
-    def sums(j):
-        return a("pb%d" % (c1[j] // 512 % 7), c1[j] % 512, c1[j] % 512 + N1[j])
+    def block(fin, banks, col, n):
+        k = max(k for k in range(len(fin) - 1) if fin[k] <= col)
+        return pb(banks[k], col - fin[k], col - fin[k] + n)
 
-    def whole(j):
-        n0 = c1[j] // 512 * 512
-        return n0, c1[j + 1], a(sums(j)[0], 0, c1[j + 1] - n0)
+    cb = gathers("b", NB, "G", VW, "invU")
+    finish("b", FINB, BANKB, "wc1", "uc1", "win", 0)
 
-    def sum1(j):
-        first = c1[j] % 512 == 0 and "u%d" % (c1[j] // 512) not in opened
-        mm(sums(j), a("NegR"), a("G", c1[j], c1[j + 1]), first, c1[j + 1] % 512 == 0 or j == len(N1) - 1)
+    def turned_sums(c, fin, banks, j):
+        for b in range(c[j] // 128, c[j + 1] // 128):
+            mm(block(fin, banks, 16 * b, 16), a("G", 128 * b, 128 * b + 128), a("NegR", 0, 16))
 
-    def wslot():
-        gat("s", a("wslot"), a("wrep"), a("LU", 0, 24))
-        compact_copy("wc", "wrep", "dwc")
-        scp(a("KlF"), a("KlB"))
+    def repeat(q, k):
+        p = 128 - 16 * k
+        for dst, src in ((slice(0, p), slice(16 * k, 128)), (slice(p, 128), slice(0, 16 * k))):
+            dma(q, "drep", T.win[dst, CD * k:CD * k + CD], T.win[src, 0:CD], R=[a("win", 0, CD)], W=[a("win", CD * k, CD * k + CD)])
 
-    run(ORDER2, {
-        "v": lambda j: gtt(a("G", c1[j], c1[j + 1]), VW, a("invU", c1[j] // 16, c1[j + 1] // 16), a("wrep", c1[j], c1[j + 1]),
-                           A.mult),
-        "k": sum1,
-        "u": uadd,
-        "e": lambda j: scp(a("win", *whole(j)[:2]), whole(j)[2]),
-        "a": lambda j: tt(a("win", *whole(j)[:2]), whole(j)[2], a("uwin", *whole(j)[:2]), A.add),
-        "slots": lambda: gat("s", a("S1"), VW, a("clU")),
-        "message": lambda: [message(k) for k in range(3)],
-        "send": lambda: send(1, scp),
+    def tot(k):
+        return pb(BANKT[k], 0, 128)
+
+    step.update({
+        "bk": lambda j: turned_sums(cb, FINB, BANKB, j),
+        "repy": lambda k: repeat("y", k),
+        "reps": lambda k: repeat("s", k),
+        "pv": lambda j: gtt(a("G", cp[j], cp[j + 1]), VW, a("invU", cp[j] // 16, cp[j + 1] // 16), a("wrep", cp[j], cp[j + 1]), A.mult),
+        "pk": lambda j: mm(sums(j), NEG, a("G", cp[j], cp[j + 1]), "u%d" % j not in ORDER.split(), True),
+        "ps": lambda j: copy("s", a("win", cp[j], cp[j + 1]), sums(j)),
+        "pc": lambda j: copy("v", a("win", cp[j], cp[j + 1]), sums(j)),
+        "pa": lambda j: tt(a("win", cp[j], cp[j + 1]), sums(j), a("uwin", cp[j], cp[j + 1]), A.add),
+        "sls": lambda k: gat("s", part("S1", k), VW, third("clU", k)),
+        "slv": lambda k: gat("v", part("S1", k), VW, third("clU", k)),
+        "slw": lambda k: gtt(part("S1", k), VW, third("clU", k), part("wslot", k), A.mult),
+        "msg": message,
+        "send": lambda: send(1, "s"),
+        "sendv": lambda: send(1, "v"),
         "consts": consts,
-        "dumps": dumps,
-        "out": conn_out,
-        "places": conn_places,
-        "mark": conn_mark,
+        "dumps": lambda: copy("s", a("dmpS"), a("dmpS"), 16.0 / (E - 1)),
+        "out": staged(conn_out()),
+        "places": staged(conn_places()),
+        "mark": lambda k: sca("s", a("Ws"), a("cnU", 8 * k, 8 * k + 8), part("ids", k)),
+        "markv": lambda k: sca("v", a("Ws"), a("cnU", 8 * k, 8 * k + 8), part("ids", k)),
+        "back": lambda: dma("y", "dc2", T.piT[:], T.Ws[0:128:16, 0:E], R=[a("Ws")], W=[a("piT")]),
         "conn": lambda: ts(a("piU"), a("piT"), 0.25, A.add),
         "uslot": lambda: gat("s", a("uslot"), a("uwin"), a("LU", 0, 24)),
-        "wslot": wslot,
+        "uslotv": lambda: gat("v", a("uslot"), a("uwin"), a("LU", 0, 24)),
+        "wslot": lambda: gat("s", a("wslot"), a("wrep"), a("LU", 0, 24), -1.0 if EARLY else 1.0),
+        "wslotv": lambda: gat("v", a("wslot"), a("wrep"), a("LU", 0, 24), -1.0 if EARLY else 1.0),
+        "klf": lambda: copy("s", a("KlF"), a("KlB")),
+        "klfv": lambda: copy("v", a("KlF"), a("KlB")),
         "arrive": lambda: arrive(1),
-        "turn": lambda: scp(a("Rw"), a("pb7", 128, 256), P=64),
-        "add": lambda: sca(a("ADD"), a("shU"), a("Rw")),
-        "total": lambda: gtt(a("D1"), a("ADD"), a("LU", 0, 24), a("S1"), A.subtract),
-        "sum": lambda: mm(a("pb3", 0, 384), a("NegR"), a("D1")),
-        "scale": lambda: tt(a("pb3", 0, 384), a("pb3", 0, 384), a("wslot"), A.mult),
-        "slot": lambda: tt(a("win", M, M + 384), a("uslot"), a("pb3", 0, 384), A.subtract),
-    })
-    compact_copy("x2c", "win", "dx2")
-
-    step = elements(R2, "X2", a("win"), "piU", "KlF", (0, 1, 2, 3))
-    step.update({
-        "order": lambda: gat("s", a("invG"), a("invF"), a("pmU")),
+        "turn": lambda: copy("s", a("Rw", 8, 136), pb(7, 128, 256), -1.0 if MATCH and not EARLY else 1.0, P=64),
+        "turnv": lambda: copy("v", a("Rw", 8, 136), pb(7, 128, 256), -1.0 if MATCH and not EARLY else 1.0, P=64),
+        "note": lambda: sca("v", a("ADD"), SH, part("ids", 0), M - 8, -1.0),
+        "find": lambda k: gtt(part("O1", k), a("ADD"), third("LU", k), NEG, A.mult),
+        "match": staged(diagonal(a("O1"), a("msk"), a("mtU"), 1.0, 0.25)),
+        "add": lambda: sca("v", a("ADD"), SH, a("Rw", 8, 136)),
+        "whole": lambda: gtt(a("D1"), a("ADD"), a("LU", 0, 24), a("S1"), A.subtract),
+        "sums": lambda: mm(pb(BANKT[0], 0, 384), NEG, a("D1")),
+        "scale": lambda: tt(pb(BANKT[0], 0, 384), pb(BANKT[0], 0, 384), a("wslot"), A.mult),
+        "slot": lambda: tt(a("win", M, M + 384), a("uslot"), pb(BANKT[0], 0, 384), A.subtract),
+        "tu": lambda k: mm(tot(k), a("IdB"), part("uslot", k), True, False),
+        "ownw": lambda k: gtt(part("S2", k), VW, third("clU", k), part("wslot", k), A.mult),
+        "own": lambda k: mm(tot(k), NEG, part("S2", k), False, False),
+        "total": lambda k: gtt(part("D1", k), a("Rw"), third("mtU", k), part("S1" if EARLY else "wslot", k),
+                               A.subtract if EARLY else A.mult),
+        "sum": lambda k: mm(tot(k), NEG, part("D1", k), False, True),
+        "fins": lambda k: copy("s", a("win", M + 128 * k, M + 128 * k + 128), tot(k)),
+        "finv": lambda k: copy("v", a("win", M + 128 * k, M + 128 * k + 128), tot(k)),
+        "wc": lambda: compact_copy("wc", "wrep", "dwc"),
+        "x2c": lambda: compact_copy("x2c", "win", "dx2"),
+        "order": lambda: gat("s", a("invG"), a("invF"), a("pmU", 0, 20)),
         "invP": lambda: ts(a("invP"), a("invG"), -1.0, A.mult, E + 0.25, A.add),
-        "compact": compact,
-        "mark": y_mark,
+        "invQ": lambda: columns(a("invP"), a("invF"), a("pmU", 0, 20)),
+        "compact": staged(compact()),
+        "ymark": lambda k: sca("v", a("Wc"), a("cpU", 8 * k, 8 * k + 8), part("ids", k), -M),
+        "yback": lambda: dma("y", "dc3", T.yF[:], T.Wc[0:128:16, 0:CB], R=[a("Wc")], W=[a("yF")]),
         "ylist": lambda: ts(a("yU"), a("yF"), 0.25, A.add),
     })
-    run(ORDER3, step)
 
-    c2 = cuts(N2)
+    cd = gathers("d", ND2, "G", VW, "invP")
+    BANKD = (0, 1, 2, 3)
+    finish("d", FIND, BANKD, "wc", "x2c", "Y", 384)
 
-    def slots():
-        for k in range(3):
-            gtt(part("S1", k), VW, a("clU", 8 * k, 8 * k + 8), part("wslot", k), A.mult)
-            message(k)
+    def pick_y(q, k):
+        hi = min(f for f in FIND if f >= OUT[k + 1])
+        gat(q, a("yc", OUT[k], OUT[k + 1]), a("Y", 0, 384 + hi), a("yU", OUT[k] // 16, OUT[k + 1] // 16))
 
-    def sum2(j):
-        for b in range(c2[j] // 128, c2[j + 1] // 128):
-            k = max(k for k in range(len(FIN) - 1) if FIN[k] <= 16 * b)
-            o = 16 * b - FIN[k]
-            mm(a("pb%d" % k, o, o + 16), a("G", 128 * b, 128 * b + 128), a("NegR", 0, 16))
+    def store(k):
+        lo, hi = STORE[k], STORE[k + 1]
+        for c in range(8):
+            n0 = place(c)
+            n = min(hi, M - n0)
+            if n > lo:
+                dma("y" if c % 2 == 0 or hi < CB else "s", "dy", T.y[:, n0 + lo:n0 + n], T.yc[16 * c:16 * c + 16, lo:n],
+                    R=[a("yc", lo, hi)])
 
-    def turned(k):
-        return a("pb%d" % k, 256, 256 + FIN[k + 1] - FIN[k])
-
-    def rows(k):
-        s = a("pb%d" % k, 0, FIN[k + 1] - FIN[k])
-        op("v", lambda e: e.transpose(ap(turned(k)), ap(s)), R=[s], W=[turned(k)])
-
-    run(ORDER4, {
-        "s": lambda j: gat("s", a("G", c2[j], c2[j + 1]), VW, a("invP", c2[j] // 16, c2[j + 1] // 16)),
-        "v": lambda j: gat("v", a("G", c2[j], c2[j + 1]), VW, a("invP", c2[j] // 16, c2[j + 1] // 16)),
-        "k": sum2,
-        "t": rows,
-        "w": lambda k: tt(turned(k), turned(k), a("wc", FIN[k], FIN[k + 1]), A.mult),
-        "x": lambda k: tt(a("Y", FIN[k], FIN[k + 1]), turned(k), a("x2c", FIN[k], FIN[k + 1]), A.add),
-        "slots": slots,
-        "send": lambda: send(2, cp),
-        "sends": lambda: send(2, scp),
-        "arrive": lambda: arrive(2),
-        "turn": lambda: cp(a("Rw"), a("pb7", 128, 256), P=64),
-        "turns": lambda: scp(a("Rw"), a("pb7", 128, 256), P=64),
-        "add": lambda: sca(a("ADD"), a("shU"), a("Rw")),
-        "total": total,
-        "sum": lambda k: mm(a("pb%d" % (4 + k), 0, 128), a("NegR"), part("D1", k)),
-        "slot": lambda k: tt(a("Y", CB + 128 * k, CB + 128 * k + 128), a("win", M + 128 * k, M + 128 * k + 128),
-                             a("pb%d" % (4 + k), 0, 128), A.subtract),
+    step.update({
+        "dk": lambda j: turned_sums(cd, FIND, BANKD, j),
+        "dslot": step["slw"],
+        "dsend": lambda: send(2, "s"),
+        "dsendv": lambda: send(2, "v"),
+        "darrive": lambda: arrive(2),
+        "dturn": lambda: copy("s", a("Rw", 8, 136), pb(7, 128, 256), P=64),
+        "dturnv": lambda: copy("v", a("Rw", 8, 136), pb(7, 128, 256), P=64),
+        "dadd": step["add"],
+        "dmsg": message,
+        "dtotal": lambda k: gtt(part("D1", k), a("Rw" if MATCH else "ADD"), third("mtU" if MATCH else "LU", k), part("S1", k), A.subtract),
+        "dsum": lambda k: mm(pb(4 + k, 0, 128), NEG, part("D1", k)),
+        "dfin": lambda k: tt(part("Y", k), a("win", M + 128 * k, M + 128 * k + 128), pb(4 + k, 0, 128), A.add if EARLY else A.subtract),
+        "yv": lambda k: pick_y("v", k),
+        "ys": lambda k: pick_y("s", k),
+        "store": store,
     })
-    gat("v", a("x2c", 0, CB // 2), a("Y"), a("yU", 0, CB // 32))
-    gat("s", a("x2c", CB // 2, CB), a("Y"), a("yU", CB // 32, CB // 16))
-    for c in range(8):
-        n0 = place(c)
-        n = min(CB, M - n0)
-        dma("y" if c % 2 == 0 else "s", "dy", T.y[:, n0:n0 + n], T.x2c[16 * c:16 * c + 16, 0:n], R=[a("x2c")])
+
+    for w in ORDER.split():
+        name = w if w in step else w.rstrip("0123456789")
+        if name == w:
+            step[w]()
+        else:
+            step[name](int(w[len(name):]))
 
     wait("g", [(name, count[name]) for name in sorted(count)])

import numpy as np
from concourse.bass import DstId, RemoteDMATransfer
from concourse.mybir import dt, AluOpType, AxisListType, ActivationFunctionType

A = AluOpType
F = ActivationFunctionType
E, M, CAPP = 4096, 4928, 128
MW = M + CAPP
RUN = MW // 16
ES = 2240
D0 = 512
SC = 1024
CB = 640
CD = 352
ND = 8 * CD
ZC = 632
PER = 4
SD = (0, 2048, E)
WT = ((0, 1536), (1536, M))
WP = ((0, 1536), (1536, 3072), (3072, M))

NA = [512, 512, 256, 256] + [512] * 4 + [256, 256]
NB = [128, 384, 512, 512, 512, 256, 256, 256]
FINB = (0, 192, 288, 352)
BANKB = (4, 5, 6)
NP = [512, 512, 512, 320, 256]
BANKP = (0, 1, 2, 3, 5)
BANKT = (4, 6, 0)
EARLY = False
MATCH = False
NC = [128, 128, 256] + [512] * 6 + [256, 256]
ND2 = [512, 256, 512, 512, 512, 512, 512, 512, 512, 512, 256]
FIND = (0, 224, 416, 544, 640)
OUT = (0, 320, 640)
STORE = (0, 640)
ORDER = (
    "ld sts oneB fz oneF fv fills datA datB key zsy runA0 runA1 runA2 warm zvy shy wy uy0 uy1 stT uy2 uy3 liy stA gAb gas abT negs keT datD datG gBf gIdF gdmp grow zero3 zero4 gIdB gAc zero5 gids grr zero0 zero7 zero1 ybs runB0 kron connU runB1 klb runB2 scatV0 shF scatV1 scatS0 scatS1 tables stB handS handV wT as0 as1 av4 av2 lists ak0 ak2 am0 am2 ak1 as3 ak3 am1 as5 ak5 ak4 uc wP0 out wD wd wP1 am4 am3 am5 addS addV as6 as7 as8 ak7 invF mask dumps as9 uslot am7 ak6 am6 invU u2 u0 ak8 u1 flag ak9 pick am8 invD am9 group keep bv0 bk0 u3 bs7 slots message bv2 bs1 bs3 bk1 bs4 bk2 bk3 bk4 sendv bv5 places pv0 bk5 bt0 bv6 bw0 bk6 mark0 mark1 mark2 back zero2 zero6 bk7 bt1 bx0 bw1 bx1 bt2 bw2 bx2 pk0 pv2 pk2 reps4 wslot order pv4 pv1 arrive turnv pk4 pk1 add total sum consts pv3 conn scale slot pa4 pk3 repy1 repy6 reps2 repy5 repy3 repy7 klf ps0 ps1 ps2 ps3 cs1 cs3 cv0 ck0 ck1 cv2 ck2 ck3 cs4 cs6 cs9 cs10 cs7 cs8 cv5 cm1 cm0 ck5 compact cm2 ymark0 cm5 ck6 ck9 cm3 ymark1 cm6 ck4 cm9 cm4 ymark2 ck7 cm7 invP ck8 cm8 wc yback x2c ck10 cm10 dslot0 ds1 dk1 dslot1 dslot2 ds0 dv2 dk0 dsend ds8 dk2 ds5 ds4 ds6 ds10 ds9 dv3 dk8 dk3 dv7 dt0 dk7 dw0 ylist dt2 dk5 darrive dx0 dw2 dx2 dturnv dadd dk4 dk6 dtotal1 dk10 dsum1 dk9 dtotal2 dt1 dtotal0 dw1 dfin1 dx1 dt3 dsum0 dw3 dfin0 dx3 dsum2 dfin2 yv0 ys1 store0")
CD = 0
ND = 8 * CD
ES = 2016
NB = []
FINB = (0,)
BANKB = ()
NP = [256, 256] + [512] * 8 + [320]
BANKP = (0, 1, 2, 3, 4, 5, 6, 0, 1, 2, 3)
BANKT = (4, 5, 6)
ORDER = "ld key sts fz zss zvs shy wy uy0 uy1 uy2 uy3 stT wT0 liy stA datA fv warm oneB oneF fills datB gAb gas datG datD grow gIdF gIdB gAc gBf grr gids gdmp zero0 zero1 zero5 zero2 zero7 zero3 zero4 abT neg runA0 runA1 runA2 keT yb kron runB0 shF runB1 connU runB2 klb scatS0 scatS1 scatV0 scatV1 handS handV wT1 stB wP0 wP1 wP2 tables as0 ak0 as1 ak1 addS lists av2 as3 am0 as4 mask ak3 ak2 am1 as5 addV am2 am3 invU invF ak4 am4 pick ak5 am5 u0 u1 flag as6 ak6 out am6 group as7 u3 ak7 as8 ak8 keep u2 as9 ak9 am7 am8 am9 uslot sls0 sls1 sls2 pv0 u5 u6 u4 pv2 msg0 pk0 msg1 msg2 send pk2 pv3 ps0 wslot ps2 dumps klf pk3 pv1 u7 pk1 pv5 pv4 pv8 places ownw2 zero6 consts pk5 pv6 pv10 pv9 pv7 ps1 u9 u8 pk4 pk8 ps5 mark0 pk6 tu1 ps4 tu0 pk9 mark1 mark2 ps3 ps6 ps9 back note ownw0 find1 find0 find2 ownw1 match pk7 tu2 arrive own0 own2 pk10 own1 turn total0 total1 total2 sum0 pa10 conn sum1 finv1 sum2 finv2 ps8 ps7 fins0 cv1 cv0 ck1 ck0 cs2 ck2 cm0 cs3 ck3 cm1 cm2 compact cs4 ck4 cm3 ymark0 cs5 ck5 cm4 ymark1 cs6 ck6 cm5 ymark2 yback x2c wc cs7 ck7 cm6 cs8 ck8 order cm7 invP cs9 ck9 cm8 cs10 ck10 cm9 cm10 dslot0 dslot1 dslot2 ds0 ylist dsendv dv1 ds2 dk0 ds4 dk1 dk2 dv3 dk3 dv5 dk4 ds6 dk5 dk6 dt0 dw0 dv8 dx0 dt1 dw1 dx1 ds7 ds10 dk8 darrive dturnv ds9 dk7 dk10 dk9 dtotal0 dtotal1 dt2 dtotal2 dw2 dsum0 dsum2 dsum1 dx2 dt3 dfin0 dw3 dfin2 dx3 dfin1 yv0 ys1 store0"
CD = 320
ND = 8 * CD
ES = 2112
NB = [128, 384, 512, 512, 512, 256, 256]
FINB = (0, 192, 320)
BANKB = (5, 6)
NP = [512, 512, 512, 512, 320]
BANKP = (0, 1, 2, 3, 4)
BANKT = (5, 6, 0)
WT = ((0, M),)
WP = ((2560, 3584), (3584, M), (0, 2560))
ORDER = "ld fz fv oneB fills shs kes zsy sty datA zvy gas gAb uy0 us1 warm stT keT abT us2 ybs uy3 negs stA runA0 datB runA1 runB0 runA2 scatS0 runB1 shF oneF runB2 datD datG grow gIdB gBf gIdF gdmp gAc zero7 zero1 zero5 grr gids zero3 zero2 zero4 connU kron scatV0 klb scatV1 scatS1 handS handV liy wy as0 stB uc wT0 wP0 wP1 wd wP2 u1 tables ak0 av1 av2 ak1 ak2 addS as5 as3 as4 as6 lists0 am0 ak3 lists1 am1 am2 lists2 am3 addV invF mask ak4 am4 invU invD pick as7 as8 as9 dumps ak5 flag ak6 u2 group am5 am6 ak8 u0 ak9 ak7 keep0 am8 am9 am7 keep1 sls0 sls1 places0 slv2 bv0 out0 u4 msg0 msg1 msg2 bk0 bs4 bs5 bk4 bk5 sendv bs6 bk6 zero0 zero6 bs1 consts bs3 bv2 pv1 places1 out1 bt1 places2 pv0 bk1 bk2 bk3 out2 bw1 places3 bt0 uslot wslot order klf places4 bw0 bx1 bx0 repy3 repy7 repy5 reps2 pk1 pk0 u3 arrive mark0 turn mark1 reps6 mark2 pv3 pk3 pv2 ps0 ps1 ps3 pk2 back repy4 repy1 add whole pv4 pc2 sums pk4 ps4 scale conn slot cv1 cs2 ck1 cs3 cv0 compact0 cm1 compact1 cv5 ck2 ck0 ck3 compact2 ck5 cm2 compact3 cm3 invP cm0 compact4 cm5 ymark0 cs7 cs4 cs9 ck7 ck4 ck9 cm7 cm4 ymark1 cm9 cs6 cs8 cs10 ck6 cm6 ymark2 x2c wc yback ck8 cm8 ck10 cm10 dslot0 dslot1 dslot2 dmsg0 dmsg1 dmsg2 ds0 dv1 dsendv ds2 dk0 dk1 dk2 dv3 dk3 dv5 dt0 ylist dw0 dv8 ds4 dk4 ds6 ds10 ds7 ds9 dk5 dk6 darrive dx0 dt1 dturnv dw1 dadd dk10 dk7 dk8 dk9 dx1 dtotal2 dtotal0 dt2 dtotal1 dt3 dw2 dsum2 dsum1 dsum0 dfin2 dw3 dx2 dfin1 dx3 dfin0 yv0 ys1 store0"

_F = "float32 "
_B = "bfloat16 "
_I = "int32 "
_U = "uint16 "
_SB = [
    (256, _I + "connI piI " + _U + "connU piU " + _F + "piT " + _B + "oneB"),
    (MW, _B + "uwin wrep " + _F + "Wv Ws ADD"), (M + 384, _F + "win"),
    (E, _B + "strep X1 " + _F + "X2"), (ES, _F + "dat"), (E + 16, _F + "V"), (8 * CB, _F + "G"),
    (RUN, _F + "zero invV invS invF"), (320, _U + "invU invP " + _F + "invG"),
    (128, _F + "oneF NegR IdF KlF Bf frow frowA frowB " + _B + "IdB asB Yb KlB"), (136, _F + "Rw"),
    (2, _F + "base rot"), (8, _B + "keB"), (20, _F + "m2"), (40, _U + "pmU"),
    (24, _F + "sh3F dmp dmpS c1 c2 c3 d1 d2 d3 " + _I + "sh3 gid low blk " + _U + "clU cnU cpU mtU"), (80, _I + "LI " + _U + "LU"),
    (384, _F + "msk O1 O2 rr ids wslot S1 S2 D1 " + _B + "Ab uslot"), (48, _F + "send1 send2"), (64, _F + "recv1 recv2"),
    (CD + 32, _B + "uc1 wc1"),
    (CB, _B + "wc " + _F + "x2c yc"), (CB + 240, _F + "Wc"), (CB + 384, _F + "Y"), (CB // 16, _F + "yF " + _U + "yU"),
]
SCRATCH = {}
for _n, _names in _SB:
    _t = ""
    for _w in _names.split():
        if _w + " " in (_F, _B, _I, _U):
            _t = _w
        else:
            SCRATCH[_w] = ("sbuf", [128, _n], _t)
for _k in range(8):
    SCRATCH["pb%d" % _k] = ("psum", [128, 512], "float32")

SEMAPHORES = ["cv", "cs", "ct", "cg", "dconn", "dshare", "dke", "du", "dWs", "dWv", "dsh", "ds1", "ds2", "ds3", "ds4",
              "dw1", "dw2", "dw3", "dw4", "dw5", "dw6", "dxv", "dxs", "dwc", "dx2", "dc1", "dc2", "dc3", "duc", "dwd", "drep",
              "dy", "arr1", "arr2", "loc1", "loc2"]


def rank_program(g, core, T, topo):
    r = T.rank_of(core)
    if r is None:
        return
    partners = [q for q in range(len(T.cores)) if q != r]
    queue = {"v": g.vector, "s": g.scalar, "t": g.tensor, "g": g, "y": g.sync}
    count = {}
    seen = {}
    past = {}

    def wait(q, toks):
        best = {}
        for name, val in toks:
            best[name] = max(best.get(name, 0), val)
        for name in sorted(best):
            if seen.get((q, name), 0) < best[name]:
                queue[q].wait_ge(T.sem[name], int(best[name]))
                seen[(q, name)] = best[name]

    def needs(q, R, W, own, acc):
        toks = []
        for lst, wr in ((R, False), (W, True)):
            for name, lo, hi in lst:
                psum = name[:2] == "pb"
                for (l2, h2, w2, sem, val, q2) in past.get(name, []):
                    if sem == own and own[:1] == "d":
                        continue
                    same = q2 == q and sem[:1] == "c"
                    if psum and not same:
                        hit = True
                    else:
                        hit = l2 < hi and lo < h2 and (w2 or wr)
                        if same and wr and acc:
                            hit = False
                    if hit:
                        toks.append((sem, count[sem] if sem[:1] == "d" else val))
        return toks

    def record(q, R, W, sem, val):
        for lst, wr in ((R, False), (W, True)):
            for name, lo, hi in lst:
                old = past.get(name, [])
                if name[:2] == "pb":
                    old = [a for a in old if a[5] == q]
                elif wr:
                    old = [a for a in old if not (lo <= a[0] and a[1] <= hi and not (a[3] == sem and sem[:1] == "d"))]
                past[name] = old + [(lo, hi, wr, sem, val, q)]

    def op(q, fn, R=(), W=(), acc=False, extra=()):
        sem = "c" + q
        wait(q, needs(q, R, W, sem, acc) + list(extra))
        fn(queue[q]).then_inc(T.sem[sem], 1)
        count[sem] = count.get(sem, 0) + 1
        record(q, R, W, sem, count[sem])

    def dma(q, sem, out, in_, R=(), W=()):
        wait(q, needs(q, R, W, sem, False))
        queue[q].dma_start(out, in_).then_inc(T.sem[sem], 16)
        count[sem] = count.get(sem, 0) + 16
        record(q, R, W, sem, count[sem])

    def a(name, lo=0, hi=None):
        return (name, lo, SCRATCH[name][1][1] if hi is None else hi)

    def ap(x, P=128):
        return T[x[0]][0:P, x[1]:x[2]]

    def pb(k, lo, hi):
        return ("pb%d" % k, lo, hi)

    def fill(x, val):
        op("v", lambda e: e.memset(ap(x), val), W=[x])

    def ts(out, in0, s1, op0, s2=None, op1=None, R=(), P=128):
        if op1 is None:
            op("v", lambda e: e.tensor_scalar(ap(out, P), ap(in0, P), s1, None, op0), R=[in0] + list(R), W=[out])
        else:
            op("v", lambda e: e.tensor_scalar(ap(out, P), ap(in0, P), s1, s2, op0, op1), R=[in0] + list(R), W=[out])

    def tt(out, in0, in1, o, P=128):
        op("v", lambda e: e.tensor_tensor(ap(out, P), ap(in0, P), ap(in1, P), o), R=[in0, in1], W=[out])

    def copy(q, out, in_, scale=1.0, P=128):
        if q == "v" and scale != 1.0:
            ts(out, in_, scale, A.mult, P=P)
        elif q == "v":
            op("v", lambda e: e.tensor_copy(ap(out, P), ap(in_, P)), R=[in_], W=[out])
        else:
            op("s", lambda e: e.activation(ap(out, P), ap(in_, P), F.Copy, scale=scale), R=[in_], W=[out])

    def silu(out, in_, bias=0.0):
        op("s", lambda e: e.activation(ap(out), ap(in_), F.Silu, bias=bias), R=[in_], W=[out])

    def gat(q, out, win, off, scale=1.0):
        if q == "v" and scale != 1.0:
            op("v", lambda e: e.tensor_scalar(ap(out), ap(win).indirect(ap(off)), scale, None, A.mult), R=[win, off], W=[out])
        elif q == "v":
            op("v", lambda e: e.tensor_copy(ap(out), ap(win).indirect(ap(off))), R=[win, off], W=[out])
        else:
            op("s", lambda e: e.activation(ap(out), ap(win).indirect(ap(off)), F.Copy, scale=scale), R=[win, off], W=[out])

    def gtt(out, win, off, in1, o):
        op("v", lambda e: e.tensor_tensor(ap(out), ap(win).indirect(ap(off)), ap(in1), o), R=[win, off, in1], W=[out])

    def columns(out, win, off):
        op("v", lambda e: e.tensor_scalar(ap(out), ap(win).indirect(ap(off)), -1.0, E + 0.25, A.mult, A.add), R=[win, off], W=[out])

    def sca(q, win, off, in_, add=None, times=1.0):
        if q == "s":
            op("s", lambda e: e.activation(ap(win).indirect(ap(off)), ap(in_), F.Silu), R=[off, in_], W=[win])
        elif add is None:
            op("v", lambda e: e.tensor_copy(ap(win).indirect(ap(off)), ap(in_)), R=[off, in_], W=[win])
        else:
            op("v", lambda e: e.tensor_scalar(ap(win).indirect(ap(off)), ap(in_), times, float(add), A.mult, A.add),
               R=[off, in_], W=[win])

    def mm(out, lhsT, rhs, start=True, stop=True, K=128, P=128, extra=()):
        op("t", lambda e: e.matmul(ap(out, P), ap(lhsT, K), ap(rhs, K), start, stop), R=[lhsT, rhs], W=[out], acc=not start,
           extra=extra)

    moved = [False]

    def gop(fn, R, W, shift):
        op("g", fn, R=R, W=W, extra=[("cg", count.get("cg", 0))] if shift or moved[0] else [])
        moved[0] = shift

    def iota(out, pattern, base, cm, p0=0, p1=128):
        gop(lambda e: e.iota(T[out[0]][p0:p1, out[1]:out[2]], pattern, base, cm, allow_small_or_imprecise_dtypes=True),
            [], [out], p0 > 0)

    def select(out, in_, pattern, cmp, base, cm, P=128, p0=0, other=0.0):
        gop(lambda e: e.affine_select(T[out[0]][p0:p0 + P, out[1]:out[2]], T[in_[0]][p0:p0 + P, in_[1]:in_[2]], pattern, cmp,
                                      other, base, cm), [in_], [out], p0 > 0)

    def staged(calls):
        return lambda k: next(calls)

    def cuts(widths, first=0):
        c = [first]
        for n in widths:
            c.append(c[-1] + n)
        return c

    def spread(q, sem, step, nm, row, lo, hi):
        x = a(nm, lo, hi)
        if step == 0:
            for p in range(0, 128, 32):
                dma(q, sem, T[nm][p:p + 1, lo:hi], T[row][0:1, lo:hi], W=[x])
        else:
            d, n = ((32, 8), (4, 4))[step - 1]
            for m in range(1, n):
                dma(q, sem, T[nm][m * d // n:128:d, lo:hi], T[nm][0:128:d, lo:hi], R=[x], W=[x] + [(nm + "4", lo, hi)] * (step == 1))

    NEG = a("NegR")
    VW = a("V")
    SH = a("LU", 72, 80)
    cp = cuts(NP, ND)
    step = {}

    def shares(q):
        for k, p in enumerate(partners):
            dma(q, "dshare", T.sh3[0:16, 8 * k:8 * k + 8], T.share[16 * p:16 * p + 16, :], W=[a("sh3")])

    def load_u(q, k):
        for c in range(2 * k, 2 * k + 2):
            dma(q, "du", T.uwin[16 * c:16 * c + 16, 0:M], T.u[:], W=[a("uwin", 0, M)])

    for q in "ys":
        step.update({
            "ke" + q: lambda q=q: dma(q, "dke", T.keB[0:8, :], T.ke[:], W=[a("keB")]),
            "sh" + q: lambda q=q: shares(q),
            "li" + q: lambda q=q: dma(q, "dsh", T.LI[:, 72:80], T.share[:], W=[a("LI", 72, 80)]),
            "zs" + q: lambda q=q: dma(q, "dWs", T.Ws[0:128:16, :], T.zero[:], R=[a("zero")], W=[a("Ws")]),
            "zv" + q: lambda q=q: dma(q, "dWv", T.Wv[0:128:16, :], T.zero[:], R=[a("zero")], W=[a("Wv")]),
            "st" + q: lambda q=q: spread(q, "ds1", 0, "strep", "st", 0, E),
            "w" + q: lambda q=q: spread(q, "dw1", 0, "wrep", "w", 0, M),
            "u" + q: lambda k, q=q: load_u(q, k),
        })

    def numbers(lo, hi):
        iota(a("dat", lo, hi), [[-1, hi - lo]], E - lo, 0)

    def fills():
        for z in (a("recv2", 16 * r, 16 * r + 16), a("uwin", M, MW), a("wrep", M, MW)):
            fill(z, 0.0)
        fill(a("Rw"), 0.0)

    def rows():
        iota(a("frow"), [[0, 8], [40, 8], [1, 2]], 0, 0, 0, 1)
        iota(a("m2"), [[2, 20]], 0, 0, 0, 1)
        if CD:
            iota(a("frowA"), [[0, 8], [CD // 16, 2], [0, 8]], 0, 0, 0, 1)
            iota(a("frowB"), [[0, 16], [CD // 8, 4], [1, 2]], 0, 0, 0, 1)

    def blocks():
        select(a("Bf"), a("oneF"), [[-16, 8], [0, 16]], A.is_ge, 0, 1)
        select(a("Bf"), a("Bf"), [[16, 8], [0, 16]], A.is_ge, 15, -1)

    step.update({
        "ld": lambda: dma("y", "dconn", T.connI[:], T.conn[:], W=[a("connI")]),
        "stT": lambda: spread("y", "ds2", 1, "strep", "st", 0, E),
        "wT": lambda k: spread("y", "dw%d" % (2 + k), 1, "wrep", "w", *WT[k]),
        "fv": lambda: fill(a("V", E, E + 16), 0.0),
        "warm": lambda: silu(a("recv1", 16 * r, 16 * r + 16), a("V", E, E + 16)),
        "fz": lambda: fill(a("zero"), 0.0),
        "oneB": lambda: fill(a("oneB"), 1.0),
        "oneF": lambda: fill(a("oneF"), 1.0),
        "fills": fills,
        "datA": lambda: numbers(0, D0),
        "datB": lambda: ts(a("dat", D0, 2 * D0), a("dat", 0, D0), float(-D0), A.add),
        "datC": lambda: silu(a("dat", 2 * D0, 3 * D0), a("dat", 0, D0), float(-2 * D0)),
        "datG": lambda: numbers(2 * D0, 3 * D0),
        "datD": lambda: numbers(3 * D0, ES),
        "gAb": lambda: select(a("Ab", 0, 128), a("oneB", 0, 128), [[0, 8], [-1, 16]], A.is_equal, 0, 1, P=16),
        "gas": lambda: select(a("asB"), a("oneB", 0, 128), [[-1, 8], [0, 16]], A.is_equal, 0, 1, P=8),
        "grow": rows,
        "gIdF": lambda: select(a("IdF"), a("oneF"), [[-1, 128]], A.is_equal, 0, 1),
        "gIdB": lambda: select(a("IdB"), a("oneB", 0, 128), [[-1, 128]], A.is_equal, 0, 1),
        "gAc": lambda: select(a("Ab", 128, 384), a("oneB"), [[0, 16], [-1, 16]], A.is_equal, 0, 1, P=16),
        "gBf": blocks,
        "grr": lambda: iota(a("rr"), [[0, 24], [32767, 16]], 0, 0),
        "gids": lambda: iota(a("ids"), [[1, 384]], M, 0),
        "gdmp": lambda: iota(a("dmpS"), [[0, 3], [16, 8]], E, 1),
        "abT": lambda: mm(pb(0, 0, 128), a("Ab", 0, 128), a("Ab", 0, 128), K=16),
    })

    def runs(k, lo, hi):
        if k == 0:
            ts(a("piI", lo, hi), a("connI", lo, hi), 15, A.bitwise_and)
            ts(pb(6, lo, hi), a("connI", lo, hi), 1.0 / (16 * RUN - 1), A.mult)
        elif k == 1:
            tt(a("piT", lo, hi), pb(6, lo, hi), a("piI", lo, hi), A.add)
        else:
            ts(a("piU", lo, hi), a("piT", lo, hi), (16 * RUN - 1) / 16.0, A.mult, 0.25, A.add)

    cs, cv = (0, SC, ES), (ES, ES + (E - ES) // 64 * 32, E)

    def compact_u():
        for c in range(8):
            dma("y", "duc", T.uc1[16 * c:16 * c + 16, 0:CD], T.u[:, CD * c:CD * c + CD], W=[a("uc1")])

    def compact_w():
        for c in range(8):
            dma("y", "dwd", T.wc1[16 * c:16 * c + 16, 0:CD], T.wrep[0:64:4, CD * c:CD * c + CD], R=[("wrep4", 0, ND)], W=[a("wc1")])

    def tables():
        mm(pb(3, 0, 24), NEG, a("sh3F"), K=16)
        mm(pb(3, 32, 52), a("frow"), a("oneF", 0, 20), True, False, K=1)
        mm(pb(3, 32, 52), a("oneF"), a("m2"), False, True, K=1)
        if CD:
            x = pb(3, 52, 52 + CD // 32)
            mm(x, a("frowA"), a("oneF", 0, CD // 32), True, False, K=1)
            mm(x, a("frowB"), a("oneF", 0, CD // 32), False, False, K=1)
            mm(x, a("oneF"), a("m2", 0, CD // 32), False, True, K=1)
            mm(pb(3, 24, 26), a("Bf"), a("dmpS", 0, 2))

    def lists():
        if CD:
            ts(a("rot"), pb(3, 24, 26), -16.0 * E - 120, A.add, CD / 256.0, A.mult)
        ts(a("LI", 0, 24), pb(3, 0, 24), -1.0, A.mult)
        ts(a("pmU", 0, 20 + CD // 32), pb(3, 32, 52 + CD // 32), float(M // 16), A.min, 0.25, A.add)
        yield
        ts(a("LI", 24, 48), a("LI", 0, 24), 4, A.arith_shift_right)
        ts(a("LI", 48, 72), a("LI", 0, 24), 15, A.bitwise_and)
        yield
        copy("v", a("LU"), a("LI"))
        yield

    step.update({
        "runA": lambda k: runs(k, 0, ES // 16),
        "runB": lambda k: runs(k, ES // 16, E // 16),
        "neg": lambda: ts(NEG, pb(0, 0, 128), -1.0, A.mult),
        "negs": lambda: copy("s", NEG, pb(0, 0, 128), -1.0),
        "keT": lambda: mm(pb(1, 0, 128), a("keB"), a("asB"), K=8, P=8),
        "yb": lambda: ts(a("Yb"), pb(1, 0, 128), -1.0, A.mult, P=8),
        "ybs": lambda: copy("s", a("Yb"), pb(1, 0, 128), -1.0, P=8),
        "kron": lambda: mm(pb(2, 0, 128), a("asB"), a("Yb"), K=8),
        "klb": lambda: tt(a("KlB"), pb(2, 0, 128), NEG, A.mult),
        "shF": lambda: copy("v", a("sh3F"), a("sh3"), P=16),
        "connU": lambda: copy("v", a("connU"), a("connI")),
        "scatS": lambda k: sca("s", a("Ws"), a("piU", cs[k] // 16, cs[k + 1] // 16), a("dat", cs[k], cs[k + 1])),
        "scatV": lambda k: sca("v", a("Wv"), a("piU", cv[k] // 16, cv[k + 1] // 16), a("dat", 0, cv[k + 1] - cv[k]), -cv[k]),
        "handS": lambda: dma("y", "dxs", T.invS[:], T.Ws[0:128:16, :], R=[a("Ws")], W=[a("invS")]),
        "handV": lambda: dma("y", "dxv", T.invV[:], T.Wv[0:128:16, :], R=[a("Wv")], W=[a("invV")]),
        "stA": lambda: spread("y", "ds3", 2, "strep", "st", SD[0], SD[1]),
        "stB": lambda: spread("y", "ds4", 2, "strep", "st", SD[1], SD[2]),
        "uc": compact_u,
        "wd": compact_w,
        "wP": lambda k: spread("y", "dw%d" % (4 + k), 2, "wrep", "w", *WP[k]),
        "zero": lambda k: iota(a("ADD", ZC * k, ZC * k + ZC), [[0, ZC]], 0, 0),
        "tables": tables,
        "lists": staged(lists()),
    })

    IV = pb(7, 0, RUN)
    CL = pb(7, 0, 384)

    def sums(j):
        return pb(BANKP[j], 0, NP[j])

    def diagonal(rows, tmp, out, s1, s2):
        op("v", lambda e: e.tensor_tensor_scan(ap(tmp), ap(a("rr")), ap(rows), 0.0, A.min, A.max), R=[a("rr"), rows], W=[tmp])
        yield
        op("v", lambda e: e.tensor_scalar(ap(out), T[tmp[0]][:, 15:384:16], s1, s2, A.mult, A.add), R=[tmp], W=[out])
        yield

    def gathers(ph, widths, out, win, lst):
        c = cuts(widths)
        for q in "sv":
            step[ph + q] = lambda j, q=q: gat(q, a(out, c[j], c[j + 1]), win, a(lst, c[j] // 16, c[j + 1] // 16))
        return c

    def elements(ph, widths, X, win, lst, K, banks):
        c = gathers(ph, widths, X, win, lst)

        def bank(j):
            return pb(banks[j % len(banks)], 0, widths[j])
        step[ph + "k"] = lambda j: mm(bank(j), a(K), a(X, c[j], c[j + 1]))
        step[ph + "m"] = lambda j: tt(a("V", c[j], c[j + 1]), bank(j), a("strep", c[j], c[j + 1]), A.mult)

    elements("a", NA, "X1", a("uwin", 0, M), "connU", "KlB", (4, 5, 6))
    elements("c", NC, "X2", a("win"), "piU", "KlF", (0, 1, 2, 3))
    step.update({
        "u": lambda j: mm(sums(j), a("IdB"), a("uwin", cp[j], cp[j + 1]), True, False),
        "mask": lambda: gat("s", a("msk"), a("NegR", 0, 16), a("LU", 48, 72), -1.0 / 16384),
        "maskv": lambda: gat("v", a("msk"), a("NegR", 0, 16), a("LU", 48, 72), -1.0 / 16384),
        "addS": lambda: mm(IV, a("IdF"), a("invS"), True, False),
        "addV": lambda: mm(IV, a("IdF"), a("invV"), False, True),
        "invU": lambda: ts(a("invU", ND // 16, M // 16), pb(7, ND // 16, M // 16), -1.0, A.mult, E + 0.25, A.add),
        "invD": lambda: columns(a("invU", 0, ND // 16), a("invF"), a("pmU", 20, 20 + CD // 32)),
        "invF": lambda: copy("s", a("invF"), IV),
        "invFv": lambda: copy("v", a("invF"), IV),
        "pick": lambda: gtt(a("O1"), a("invF"), a("LU", 24, 48), a("msk"), A.mult),
        "flag": lambda: mm(CL, a("Ab", 0, 128), a("Ab"), True, False, K=16),
        "group": lambda: mm(CL, a("Bf"), a("O1"), False, True),
        "keep": staged(diagonal(CL, a("O2"), a("clU"), -16384.0, 16384 + E + 0.25)),
    })

    used, masks = [], {}
    for q in sorted(partners, key=lambda q: len(topo.engines(core, T.cores[q]))):
        ok = [e for e in topo.engines(core, T.cores[q]) if e not in used][:PER]
        used += ok
        masks[q] = sum(1 << e for e in ok)

    def part(nm, k):
        return a(nm, 128 * k, 128 * k + 128)

    def third(nm, k):
        return a(nm, 8 * k, 8 * k + 8)

    def message(k):
        mm(pb(7, 16 * k, 16 * k + 16), part("S1", k), a("NegR", 0, 16))

    def send(rnd, by):
        nm = "send%d" % rnd
        copy(by, a(nm), pb(7, 0, 48))
        wait("g", needs("g", [a(nm)], [], "loc%d" % rnd, False))
        tr = []
        for k, q in enumerate(partners):
            rid, pid, _se = topo.addr(T.cores[q])
            tr.append(RemoteDMATransfer(dst_ids=[DstId(rid=rid, pnc=pid)], dma_engine_mask=masks[q],
                                        remote_sem=T.sem["arr%d" % rnd], src=T[nm][:, 16 * k:16 * k + 16],
                                        dst=T["recv%d" % rnd][:, 16 * r:16 * r + 16]))
        g.remote_dma_fused(tr, local_sem=T.sem["loc%d" % rnd])
        count["loc%d" % rnd] = 3 * PER
        count["arr%d" % rnd] = 3 * PER

    def arrive(rnd):
        mm(pb(7, 128, 256), a("recv%d" % rnd), a("IdF"), P=64, extra=[("arr%d" % rnd, 3 * PER)])

    def place(c):
        return CB * (4 * (c % 2) + c // 2)

    def compact_copy(nm, src, sem):
        for c in range(8):
            n0 = place(c)
            n = min(CB, M - n0)
            dma("y", sem, T[nm][16 * c:16 * c + 16, 0:n], T[src][0:16, n0:n0 + n], R=[a(src, 0, M)], W=[a(nm)])

    def consts():
        iota(a("dmp"), [[0, 3], [16, 8]], CB, 1)
        iota(a("Wc", 0, CB), [[1, 16], [16, CB // 16]], 384, 0)
        for k in range(4):
            iota(a("base"), [[0, 2]], place(2 * k + 1) // 16, 0, 32 * k, 32 * k + 32)
            select(a("base"), a("base"), [[0, 2]], A.is_ge, -16, 1, 32, 32 * k, float(place(2 * k) // 16))
        for nm in ("wc", "x2c"):
            iota(a(nm, 448, CB), [[0, CB - 448]], 0, 0, 96, 128)

    def conn_out():
        x, y, rot = pb(3, 0, 256), pb(3, 256, 512), T.rot[:, 0:1]
        if CD:
            ts(x, a("connI"), float(ND), A.is_lt, rot, A.mult, R=[a("rot")])
            ts(y, a("connI"), rot, A.is_lt, float(ND), A.mult, R=[a("rot")])
            yield
            tt(a("piT"), a("connI"), x, A.subtract)
            yield
            tt(a("piT"), a("piT"), y, A.add)
        else:
            copy("v", a("piT"), a("connI"))
        dma("y", "dc1", T.Ws[0:128:16, 0:E], T.piT[:], R=[a("piT")], W=[a("Ws")])
        yield

    def conn_places():
        last = T.O2[:, 15:384:16]

        def from_last(out, s1, s2):
            op("v", lambda e: e.tensor_scalar(ap(out), last, s1, s2, A.mult, A.add), R=[a("O2")], W=[out])
        from_last(a("gid"), -16384.0, 16384.0 + E)
        from_last(a("c1"), -16384.0 / (E - 1), (16384.0 + E) / (E - 1))
        from_last(a("c2"), -2.0 ** 20, 2.0 ** 20 + 64)
        yield
        ts(a("low"), a("gid"), 15, A.bitwise_and)
        tt(a("c2"), a("c2"), a("dmpS"), A.min)
        yield
        tt(a("c1"), a("c1"), a("low"), A.add)
        yield
        tt(a("c3"), a("c1"), a("c2"), A.max)
        yield
        ts(a("cnU"), a("c3"), (E - 1) / 16.0, A.mult, 0.25, A.add)
        yield

    def compact():
        b = T.base[:, 0:1]
        ts(a("blk"), a("LI", 0, 24), 1.0 / CB, A.mult, -0.4992, A.add)
        ts(a("d1"), a("LI", 48, 72), float(CB // 16), A.mult, b, A.subtract, R=[a("base")])
        tt(a("d3"), a("LI", 24, 48), a("dmp"), A.subtract)
        yield
        ts(a("d2"), a("blk"), float(CB // 16), A.mult, b, A.is_equal, R=[a("base")])
        tt(a("d1"), a("d1"), a("d3"), A.add)
        yield
        tt(a("d1"), a("d1"), a("d2"), A.mult)
        yield
        tt(a("d1"), a("d1"), a("dmp"), A.add)
        yield
        copy("v", a("cpU"), a("d1"))
        yield

    def finish(ph, fin, banks, w, old, out, first):
        def turned(k):
            return pb(banks[k], 256, 256 + fin[k + 1] - fin[k])

        def rows(k):
            s = pb(banks[k], 0, fin[k + 1] - fin[k])
            op("v", lambda e: e.transpose(ap(turned(k)), ap(s)), R=[s], W=[turned(k)])
        step[ph + "t"] = rows
        step[ph + "w"] = lambda k: tt(turned(k), turned(k), a(w, fin[k], fin[k + 1]), A.mult)
        step[ph + "x"] = lambda k: tt(a(out, first + fin[k], first + fin[k + 1]), turned(k), a(old, fin[k], fin[k + 1]), A.add)

    def block(fin, banks, col, n):
        k = max(k for k in range(len(fin) - 1) if fin[k] <= col)
        return pb(banks[k], col - fin[k], col - fin[k] + n)

    cb = gathers("b", NB, "G", VW, "invU")
    finish("b", FINB, BANKB, "wc1", "uc1", "win", 0)

    def turned_sums(c, fin, banks, j):
        for b in range(c[j] // 128, c[j + 1] // 128):
            mm(block(fin, banks, 16 * b, 16), a("G", 128 * b, 128 * b + 128), a("NegR", 0, 16))

    def repeat(q, k):
        p = 128 - 16 * k
        for dst, src in ((slice(0, p), slice(16 * k, 128)), (slice(p, 128), slice(0, 16 * k))):
            dma(q, "drep", T.win[dst, CD * k:CD * k + CD], T.win[src, 0:CD], R=[a("win", 0, CD)], W=[a("win", CD * k, CD * k + CD)])

    def tot(k):
        return pb(BANKT[k], 0, 128)

    step.update({
        "bk": lambda j: turned_sums(cb, FINB, BANKB, j),
        "repy": lambda k: repeat("y", k),
        "reps": lambda k: repeat("s", k),
        "pv": lambda j: gtt(a("G", cp[j], cp[j + 1]), VW, a("invU", cp[j] // 16, cp[j + 1] // 16), a("wrep", cp[j], cp[j + 1]), A.mult),
        "pk": lambda j: mm(sums(j), NEG, a("G", cp[j], cp[j + 1]), "u%d" % j not in ORDER.split(), True),
        "ps": lambda j: copy("s", a("win", cp[j], cp[j + 1]), sums(j)),
        "pc": lambda j: copy("v", a("win", cp[j], cp[j + 1]), sums(j)),
        "pa": lambda j: tt(a("win", cp[j], cp[j + 1]), sums(j), a("uwin", cp[j], cp[j + 1]), A.add),
        "sls": lambda k: gat("s", part("S1", k), VW, third("clU", k)),
        "slv": lambda k: gat("v", part("S1", k), VW, third("clU", k)),
        "slw": lambda k: gtt(part("S1", k), VW, third("clU", k), part("wslot", k), A.mult),
        "msg": message,
        "send": lambda: send(1, "s"),
        "sendv": lambda: send(1, "v"),
        "consts": consts,
        "dumps": lambda: copy("s", a("dmpS"), a("dmpS"), 16.0 / (E - 1)),
        "out": staged(conn_out()),
        "places": staged(conn_places()),
        "mark": lambda k: sca("s", a("Ws"), a("cnU", 8 * k, 8 * k + 8), part("ids", k)),
        "markv": lambda k: sca("v", a("Ws"), a("cnU", 8 * k, 8 * k + 8), part("ids", k)),
        "back": lambda: dma("y", "dc2", T.piT[:], T.Ws[0:128:16, 0:E], R=[a("Ws")], W=[a("piT")]),
        "conn": lambda: ts(a("piU"), a("piT"), 0.25, A.add),
        "uslot": lambda: gat("s", a("uslot"), a("uwin"), a("LU", 0, 24)),
        "uslotv": lambda: gat("v", a("uslot"), a("uwin"), a("LU", 0, 24)),
        "wslot": lambda: gat("s", a("wslot"), a("wrep"), a("LU", 0, 24), -1.0 if EARLY else 1.0),
        "wslotv": lambda: gat("v", a("wslot"), a("wrep"), a("LU", 0, 24), -1.0 if EARLY else 1.0),
        "klf": lambda: copy("s", a("KlF"), a("KlB")),
        "klfv": lambda: copy("v", a("KlF"), a("KlB")),
        "arrive": lambda: arrive(1),
        "turn": lambda: copy("s", a("Rw", 8, 136), pb(7, 128, 256), -1.0 if MATCH and not EARLY else 1.0, P=64),
        "turnv": lambda: copy("v", a("Rw", 8, 136), pb(7, 128, 256), -1.0 if MATCH and not EARLY else 1.0, P=64),
        "note": lambda: sca("v", a("ADD"), SH, part("ids", 0), M - 8, -1.0),
        "find": lambda k: gtt(part("O1", k), a("ADD"), third("LU", k), NEG, A.mult),
        "match": staged(diagonal(a("O1"), a("msk"), a("mtU"), 1.0, 0.25)),
        "add": lambda: sca("v", a("ADD"), SH, a("Rw", 8, 136)),
        "whole": lambda: gtt(a("D1"), a("ADD"), a("LU", 0, 24), a("S1"), A.subtract),
        "sums": lambda: mm(pb(BANKT[0], 0, 384), NEG, a("D1")),
        "scale": lambda: tt(pb(BANKT[0], 0, 384), pb(BANKT[0], 0, 384), a("wslot"), A.mult),
        "slot": lambda: tt(a("win", M, M + 384), a("uslot"), pb(BANKT[0], 0, 384), A.subtract),
        "tu": lambda k: mm(tot(k), a("IdB"), part("uslot", k), True, False),
        "ownw": lambda k: gtt(part("S2", k), VW, third("clU", k), part("wslot", k), A.mult),
        "own": lambda k: mm(tot(k), NEG, part("S2", k), False, False),
        "total": lambda k: gtt(part("D1", k), a("Rw"), third("mtU", k), part("S1" if EARLY else "wslot", k),
                               A.subtract if EARLY else A.mult),
        "sum": lambda k: mm(tot(k), NEG, part("D1", k), False, True),
        "fins": lambda k: copy("s", a("win", M + 128 * k, M + 128 * k + 128), tot(k)),
        "finv": lambda k: copy("v", a("win", M + 128 * k, M + 128 * k + 128), tot(k)),
        "wc": lambda: compact_copy("wc", "wrep", "dwc"),
        "x2c": lambda: compact_copy("x2c", "win", "dx2"),
        "order": lambda: gat("s", a("invG"), a("invF"), a("pmU", 0, 20)),
        "invP": lambda: ts(a("invP"), a("invG"), -1.0, A.mult, E + 0.25, A.add),
        "invQ": lambda: columns(a("invP"), a("invF"), a("pmU", 0, 20)),
        "compact": staged(compact()),
        "ymark": lambda k: sca("v", a("Wc"), a("cpU", 8 * k, 8 * k + 8), part("ids", k), -M),
        "yback": lambda: dma("y", "dc3", T.yF[:], T.Wc[0:128:16, 0:CB], R=[a("Wc")], W=[a("yF")]),
        "ylist": lambda: ts(a("yU"), a("yF"), 0.25, A.add),
    })

    cd = gathers("d", ND2, "G", VW, "invP")
    BANKD = (0, 1, 2, 3)
    finish("d", FIND, BANKD, "wc", "x2c", "Y", 384)

    def pick_y(q, k):
        hi = min(f for f in FIND if f >= OUT[k + 1])
        gat(q, a("yc", OUT[k], OUT[k + 1]), a("Y", 0, 384 + hi), a("yU", OUT[k] // 16, OUT[k + 1] // 16))

    def store(k):
        lo, hi = STORE[k], STORE[k + 1]
        for c in range(8):
            n0 = place(c)
            n = min(hi, M - n0)
            if n > lo:
                dma("y" if c % 2 == 0 or hi < CB else "s", "dy", T.y[:, n0 + lo:n0 + n], T.yc[16 * c:16 * c + 16, lo:n],
                    R=[a("yc", lo, hi)])

    step.update({
        "dk": lambda j: turned_sums(cd, FIND, BANKD, j),
        "dslot": step["slw"],
        "dsend": lambda: send(2, "s"),
        "dsendv": lambda: send(2, "v"),
        "darrive": lambda: arrive(2),
        "dturn": lambda: copy("s", a("Rw", 8, 136), pb(7, 128, 256), P=64),
        "dturnv": lambda: copy("v", a("Rw", 8, 136), pb(7, 128, 256), P=64),
        "dadd": step["add"],
        "dmsg": message,
        "dtotal": lambda k: gtt(part("D1", k), a("Rw" if MATCH else "ADD"), third("mtU" if MATCH else "LU", k), part("S1", k), A.subtract),
        "dsum": lambda k: mm(pb(4 + k, 0, 128), NEG, part("D1", k)),
        "dfin": lambda k: tt(part("Y", k), a("win", M + 128 * k, M + 128 * k + 128), pb(4 + k, 0, 128), A.add if EARLY else A.subtract),
        "yv": lambda k: pick_y("v", k),
        "ys": lambda k: pick_y("s", k),
        "store": store,
    })

    for w in ORDER.split():
        name = w if w in step else w.rstrip("0123456789")
        if name == w:
            step[w]()
        else:
            step[name](int(w[len(name):]))

    wait("g", [(name, count[name]) for name in sorted(count)])
